import numpy as np, ml_dtypes
CORES = [30,158,46,174,86,214]
N = 6
BF = ml_dtypes.bfloat16
P, G, RO, C, J = 1024, 256, 3, 5, 2
W = P + (N - 1) * G
def parts(rng):
    w = rng.choice(np.array([4, 12, 40]), (N, 8, 1, 1))
    r = (120 * rng.random((N, 8, 1, P)) + w * rng.random((N, 8, 16, P))).astype(np.int64)
    v = (60 + 150 * rng.random((N, 8, 1, P)) + w * rng.random((N, 8, 16, P))).astype(np.int64)
    m = np.minimum(rng.poisson(0.4 + 0.35 * rng.random((N, 8, 1, 1, 16)), (N, 8, 16, 16, 16)), 15)
    low = rng.random((N, 8, 16, P)) < rng.choice(np.array([0.2, 0.5, 0.8]), (N, 8, 1, 1))
    s = np.where(low, rng.integers(0, G, low.shape), rng.integers(0, W, low.shape))
    return v, r, m, s
def pack(v, r, m, s):
    return {"v0": np.ascontiguousarray(v.reshape(N, 128, P)).astype(np.float32).astype(BF), "rew": np.ascontiguousarray(r.reshape(N, 128, P)).astype(np.float32).astype(BF),
            "mat": np.ascontiguousarray(m.reshape(N, 128, 256)).astype(np.float32).astype(BF), "succ": np.ascontiguousarray(s.reshape(N, 128, P)).astype(np.int32)}
def setup_inputs(rng):
    return pack(*parts(rng))
def near(rng, base):
    u = rng.integers(0, 4, (N, 8, 1, P)); i1 = rng.integers(0, 16, u.shape); i2 = (i1 + rng.integers(1, 16, u.shape)) % 16; st = np.arange(16)[:, None]
    return base + ((st == i1) & (u % 2 == 1)) - ((st == i2) & (u >= 2))
def setup_inputs_ties(rng):
    v, r, m, s = parts(rng); base = rng.integers(50, 201, (1, 8, 16, 1))
    r = near(rng, base); v = near(rng, base); m[:, :4] = 0; m[:, 4:6, :, 1::2] = 0; r[:, 4:] = r[:, 4:] >> 1
    return pack(v, r, m, s)
def setup_inputs_chains(rng):
    v, r, m, s = parts(rng); m[:, ::2] = 0
    o = np.argsort(rng.random((N, 8, P)), axis=-1); at = np.argsort(o, axis=-1)
    r = (at[:, :, None, :] + np.arange(16)[:, None]) >> 4; v = np.array(r)
    up = np.where(at == P - 1, rng.integers(P, W, at.shape), np.take_along_axis(o, np.minimum(at + 1, P - 1), 2)); down = np.take_along_axis(o, np.maximum(at - 1, 0), 2)
    v[0, ::4, :, :G] = P // 16 + 6
    for a in range(1, N): up[a, ::4] = np.where(at[a, ::4] == P - 1, P + (N - 1 - a) * G + up[a, ::4] % G, up[a, ::4])
    s[:, :, ::2] = up[:, :, None, :]
    s[:, 2::4, 0] = down[:, 2::4]; s[:, 3::4, 0] = down[:, 3::4]
    s[:, 2::4, 1::2] = rng.integers(G, W, s[:, 2::4, 1::2].shape)
    return pack(v, r, m, s)
def setup_inputs_alike(rng):
    v, r, m, s = parts(rng)
    s[:, 0] = rng.choice(np.array([0, P - 1, P, W - 1, G - 1, G]), (N, 16, P))
    s[:, 1] = np.arange(P)
    s[:, 2] = rng.integers(P, W, (N, 16, P))
    s[:, 3] = rng.integers(0, G, (N, 16, P))
    s[:, 4] = s[:, 4, :1]
    v[:, 5] = rng.integers(1, 200, (N, 1, 1))
    s[:, 6] = rng.integers(0, 8, (N, 16, P))
    return pack(v, r, m, s)
def setup_inputs_full(rng):
    v, r, m, s = parts(rng)
    r[:, 0] = 255
    r[:, 1] = 0; v[:, 1] = 0
    m[:, 2] = 15; v[:, 2] = rng.integers(0, 3, (N, 16, P))
    v[:, 3] = 0; v[rng.integers(0, N), 3] = 255
    v[:, 4] = 255 * rng.integers(0, 2, (N, 16, P)); r[:, 4] = rng.choice(np.array([0, 254, 255]), (N, 16, P))
    m[:, 5] = 0; m[:, 5, 0, :2] = 1; v[:, 5, 0] = rng.integers(126, 131, (N, P)); r[:, 5] = rng.integers(0, 2, (N, 16, P)); r[:, 5, 0] = rng.integers(126, 131, (N, P))
    m[:, 6] = 0; m[:, 6, :, 2] = rng.integers(13, 16, (N, 16, 16)); v[:, 6] = rng.integers(60, 241, (N, 1, P)) + rng.integers(0, 16, (N, 16, P)); r[:, 6] = rng.integers(0, 16, (N, 16, P))
    k = np.arange(16) != rng.integers(0, 16); h = rng.integers(0, 256, (N, 1, P))
    m[:, 7] = 0; m[:, 7, :, 1] = 15 * (k[:, None] == k[None, :]); v[:, 7] = np.where(k[:, None], h, 255 - h); r[:, 7] = rng.integers(0, 16, (N, 16, P))
    return pack(v, r, m, s)
def setup_inputs_spread(rng):
    v, r, m, s = parts(rng)
    v = np.minimum((np.exp2(8 * rng.random((N, 8, 1, P))) * rng.random((N, 8, 16, P))).astype(np.int64), 255)
    r = np.minimum((np.exp2(8 * rng.random((N, 8, 1, P))) * rng.random((N, 8, 16, P))).astype(np.int64), 255)
    m = np.minimum((16 * rng.random((N, 8, 16, 16, 16)) ** rng.choice(np.array([8, 16, 64]), (N, 8, 1, 1, 16))).astype(np.int64), 15)
    s = np.minimum((W * rng.random((N, 8, 16, P)) ** rng.choice(np.array([0.5, 1, 3]), (N, 8, 16, 1))).astype(np.int64), W - 1)
    return pack(v, r, m, s)
def check_inputs(d):
    bad = []
    for k, hi in (("v0", 255), ("rew", 255), ("mat", 15), ("succ", W - 1)):
        x = np.asarray(d[k]).astype(np.float64)
        if not (np.all(x >= 0) and np.all(x <= hi) and np.all(x == np.floor(x))): bad.append("whole numbers and range of " + k)
    return bad
def value(w, s, m, r):
    z = np.stack([m[g] @ np.take(w[g], s[g], axis=1).reshape(256, P) for g in range(8)])
    return np.minimum(255, r + np.floor(z * 2.0 ** -8))
def reference(v0, rew, mat, succ):
    v = v0.astype(np.float64).reshape(N, 8, 16, P); r = rew.astype(np.float64).reshape(N, 8, 16, P); s = succ.astype(np.int64).reshape(N, 8, 16, P)
    m = np.ascontiguousarray(mat.astype(np.float64).reshape(N, 8, 16, 16, 16).transpose(0, 1, 4, 2, 3)).reshape(N, 8, 16, 256)
    n = np.arange(P)
    for t in range(RO):
        nv, ns = [], []
        odd = ((np.arange(16) + t) & 1)[:, None] == 1
        for a in range(N):
            w = np.concatenate([v[a]] + [v[(a + d) % N][:, :, :G] for d in range(1, N)], axis=2)
            x = value(w, s[a], m[a], r[a])
            guest = (n + np.add.reduce(v[a], axis=1).astype(np.int64)) & (G - 1)
            e = np.take_along_axis(s[(a + t + 1) % N], guest[:, None, :], 2)
            c = np.where(odd, np.where(e < G, P + G * t + e, n), s[a])
            y = value(w, c, m[a], r[a])
            ok = np.all(y >= x, axis=1)[:, None, :]
            x = np.where(ok, y, x); c = np.where(ok, c, s[a])
            u = np.concatenate([x, w[:, :, P:]], axis=2); total = np.add.reduce(u, axis=1)
            D = np.tile(np.arange(W), (8, 1))
            for k in range(C - 1, -1, -1):
                h = c[:, 3 * k + t]
                good = np.all(np.take_along_axis(u, h[:, None, :], 2) >= x, axis=1) & (np.take_along_axis(total, h, 1) > total[:, :P])
                D[:, :P] = np.where(good, h, D[:, :P])
            for _ in range(J): D = np.take_along_axis(D, D, 1)
            nv.append(x); ns.append(np.take_along_axis(D, c.reshape(8, 16 * P), 1).reshape(8, 16, P))
        v = np.stack(nv); s = np.stack(ns)
    return {"yv": v.reshape(N, 128, P).astype(np.float32).astype(BF), "ys": s.reshape(N, 128, P).astype(np.float32)}

@@ -1,0 +1,579 @@
+from concourse.bass import DstId, RemoteDMATransfer
+from concourse.mybir import AluOpType, ActivationFunctionType
+
+ALU = AluOpType
+ACT = ActivationFunctionType
+P, GH, NR, RO = 1024, 256, 6, 3
+OWN = [0, 2304, 3328]
+WIN = [2304, 3328, 4352]
+OFF16 = 1664
+
+bf, f32, i32, u16, f16 = "bfloat16", "float32", "int32", "uint16", "float16"
+SCRATCH = {"MB": ("sbuf", [128, 16, 8, 16], bf)}
+for _dt, _list in (
+        (bf, "W0 2304 W1 3328 W2 5632 UW 5632 FT 5632 DTa 2304 DTb 2304 HL 2304 GA 16384 GB 8192 GS 2048 RW 1024 MT 256 LT 1024 "
+             "DF0 1024 DF1 1024 DF2 1024 DF3 1024 DF4 1024 SG0 1024 SG1 1024 E 128 ID 128 LM 128 NL 128 PEN 128 ZB 144 ZK 144 ZH 144 "
+             "CH 512 CN 96 CB1 256 CB2 256 VN 1024"),
+        (f32, "SW0 2048 SW1 2048 X0 1024 X1 1024 X2 1024 TG0 256 TG1 256 TG2 256 TS0 256 TS1 256 TS2 256 TM 256 TV 256 C2f 512 "
+              "SNf 128 YS 1024 COL 16 GM 8 Z32 288 IL 64 OA 64 OB 64 KY 320 ZZ 320 AC 384 LC 64 LD 64"),
+        (i32, "SI 1024 AI 1024 IK 128 IK2 128 II 128 IZ 144 IM 64 IP 8 GI 64 GJ 64 AJ 64 AK 64"),
+        (u16, "SU 1024 C2u 512 SNu 128 GL 64 OL 64 KL 320 DR 64 D1 64 LA 64 LB 64"),
+        (f16, "S16 1024 ZR 2304 B16 1024 I16 128")):
+    _w = _list.split()
+    for _k in range(0, len(_w), 2):
+        SCRATCH[_w[_k]] = ("sbuf", [128, int(_w[_k + 1])], _dt)
+PSUM = ("A0", "A1", "B0", "B1", "P4", "P5", "P6", "P7")
+for _k in PSUM:
+    SCRATCH[_k] = ("psum", [128, 512], f32)
+SEMAPHORES = (["cv", "ca", "cp", "cg"] + ["arV%d" % t for t in range(RO)] + ["arT%d" % t for t in range(RO)]
+              + ["d%d" % k for k in range(64)])
+
+CG, CPE, LAT, OVH, CDMA, CREM = 1.55, 0.55, 150.0, 70.0, 2400.0, 4500.0
+TRIES, SEED, SLACK = 25000, 3, 250.0
+ACH, BCH = 64, 64
+LAST = [(128 * j, 128) for j in range(6)] + [(768 + 64 * j, 64) for j in range(4)]
+WAYS = ["aa", "vv", "aa", "vv", "va"]
+KORD = [4, 0, 1, 2, 3]
+PLAN = {}
+
+
+def _conf(a, b):
+    return a[0] == b[0] and a[1] < b[2] and b[1] < a[2] and (a[3] is None or b[3] is None or a[3] == b[3])
+
+
+def build(g, core, T, topo):
+    rank = T.rank_of(core)
+    ops = []
+    V, S, PE = g.vector, g.scalar, g.tensor
+
+    def reg(x):
+        return x if len(x) == 4 else (x[0], x[1], x[2], None)
+
+    def op(eng, cost, fn, r, w, kind="c", after=None, sem=None, inc=1):
+        ops.append({"eng": eng, "cost": cost, "fn": fn, "r": [reg(x) for x in r], "w": [reg(x) for x in w],
+                    "kind": kind, "after": after, "sem": sem, "inc": inc})
+        return len(ops) - 1
+
+    def ap(x):
+        return T[x[0]][:, x[1]:x[2]]
+
+    def two(x):
+        return SCRATCH[x[0]][2] in (bf, u16, f16)
+
+    def ts(out, in_, s1, s2, o0, o1=None):
+        n = in_[2] - in_[1]
+        c = max(64, n * (0.5 if two(out) and two(in_) else 1.0)) + OVH
+        a1 = ap(s1) if isinstance(s1, tuple) else s1
+        if o1 is None:
+            fn = lambda e: V.tensor_scalar(ap(out), ap(in_), a1, None, o0)
+        else:
+            fn = lambda e: V.tensor_scalar(ap(out), ap(in_), a1, s2, o0, o1)
+        return op("v", c, fn, [in_] + ([s1] if isinstance(s1, tuple) else []), [out])
+
+    def cp(out, in_):
+        n = in_[2] - in_[1]
+        c = max(64, n * (0.5 if two(out) and two(in_) else 1.0)) + OVH
+        return op("v", c, lambda e: V.tensor_copy(ap(out), ap(in_)), [in_], [out])
+
+    def tt(out, a, b, o):
+        n = a[2] - a[1]
+        c = max(64, n * (1 if a[0] in PSUM or b[0] in PSUM else 2)) + OVH
+        return op("v", c, lambda e: V.tensor_tensor(ap(out), ap(a), ap(b), o), [a, b], [out])
+
+    def act(out, in_, func, bias):
+        return op("a", in_[2] - in_[1] + OVH, lambda e: S.activation(ap(out), ap(in_), func, bias=bias), [in_], [out])
+
+    def move(out, in_):
+        def fn(e):
+            if e == "v":
+                return V.tensor_copy(ap(out), ap(in_))
+            return S.activation(ap(out), ap(in_), ACT.Copy)
+        return op("va", in_[2] - in_[1] + OVH, fn, [in_], [out])
+
+    def gat(out, win, off, eng="va"):
+        def fn(e):
+            src = ap(win).indirect(ap(off))
+            if e == "v":
+                return V.tensor_copy(ap(out), src)
+            return S.activation(ap(out), src, ACT.Copy)
+        return op(eng, (out[2] - out[1]) * CG + OVH, fn, [win, off], [out])
+
+    def gat2(out, win, off):
+        for h in range(2):
+            gat((out[0], out[1] + 512 * h, out[1] + 512 * h + 512), win, (off[0], off[1] + 32 * h, off[1] + 32 * h + 32))
+
+    def gtt(out, win, off, b, o):
+        return op("v", (out[2] - out[1]) * CG + OVH,
+                  lambda e: V.tensor_tensor(ap(out), ap(win).indirect(ap(off)), ap(b), o), [win, off, b], [out])
+
+    def mm(items, r, bank, slow=1, stop=True):
+        def fn(e):
+            last = None
+            for k, (lo, hi, l, x, st) in enumerate(items):
+                last = PE.matmul(T[bank][:, lo:hi], l, x, st, stop and k == len(items) - 1)
+            return last
+        c = sum(max(64, it[1] - it[0]) for it in items) * CPE * slow + OVH
+        return op("p", c, fn, r, [(bank, min(it[0] for it in items), max(it[1] for it in items))])
+
+    def tolist(bank, lo, z, z0, src, tail=None, slow=1):
+        n = src[2] - src[1]
+        it = [(lo, lo + n // 16, T[z][:, z0 + 15 - q:z0 + 143 - q], T[src[0]][:, src[1] + q:src[2]:16], q == 0)
+              for q in range(16)]
+        r = [src, (z, z0, z0 + 144)]
+        if tail is not None:
+            it.append((lo, lo + n // 16, T.ID[:, :], ap(tail), False))
+            r += [tail, ("ID", 0, 128)]
+        return mm(it, r, bank, slow)
+
+    def dma(out, in_, r, w, eng="s"):
+        q = {"s": g.sync, "a": g.scalar}[eng]
+        return op(eng, CDMA, lambda e: q.dma_start(out, in_), r, w, kind="d", inc=16)
+
+    def pool(out, n, pattern, base, cm, w, small=False):
+        if small:
+            fn = lambda e: g.iota(out, pattern, base, cm, allow_small_or_imprecise_dtypes=True)
+        else:
+            fn = lambda e: g.iota(out, pattern, base, cm)
+        return op("g", 2 * n + 160, fn, [], [w, ("pool", 0, 1)])
+
+    def fill(x, val):
+        n = x[2] - x[1]
+        return op("v", max(64, n * (0.5 if two(x) else 1.0)) + OVH, lambda e: V.memset(ap(x), val), [], [x])
+
+    def send(src, dests, sem, land, cost):
+        mask = topo.mask(core, dests[0][0])
+        for d, _ in dests:
+            mask &= topo.mask(core, d)
+        ne = bin(mask).count("1")
+
+        def fn(e, loc):
+            ids = []
+            for d, _ in dests:
+                rid, pid = topo.addr(d, core)
+                ids.append(DstId(rid=rid, pnc=pid))
+            tr = RemoteDMATransfer(dst_ids=ids, dma_engine_mask=mask, remote_sem=T.sem[sem], src=ap(src),
+                                   dsts=[x for _, x in dests])
+            return g.remote_dma_fused([tr], local_sem=loc)
+        k = op("g", cost, fn, [src], [], kind="r", inc=ne)
+        op("x", 1, None, [], [land], kind="x", after=k, sem=sem, inc=ne * len(dests))
+
+    def send_values(t, src):
+        dests = [(T.cores[(rank - d) % NR], T["W%d" % t][:, P + (d - 1) * GH:P + d * GH]) for d in range(1, NR)]
+        send(src, dests, "arV%d" % t, ("W%d" % t, P, 2304), CREM + 2500)
+
+    def send_tuples(t):
+        send(("TS%d" % t, 0, 256), [(T.cores[(rank - t - 1) % NR], T["TG%d" % t][:, :])], "arT%d" % t,
+             ("TG%d" % t, 0, 256), CREM)
+
+    dma(T.W0[:, 0:GH], T.v0[:, 0:GH], [], [("W0", 0, GH)])
+    dma(T.SI[:, :], T.succ[:, :], [], [("SI", 0, P)], eng="a")
+    dma(T.W0[:, GH:P], T.v0[:, GH:P], [], [("W0", GH, P)])
+    dma(T.MT[:, :], T.mat[:, :], [], [("MT", 0, 256)])
+    dma(T.RW[:, :], T.rew[:, :], [], [("RW", 0, P)], eng="a")
+    pool(T.IK[:, :], 128, [[-16, 8], [0, 16]], 0, 1, ("IK", 0, 128))
+    pool(T.II[:, :], 128, [[-1, 128]], 0, 1, ("II", 0, 128))
+    pool(T.IP[:, 0:1], 1, [[0, 1]], 0, 1, ("IP", 0, 1))
+    pool(T.IM[:, :], 64, [[16, 64]], 0, 0, ("IM", 0, 64))
+    send_values(0, ("W0", 0, GH))
+    pool(T.IZ[:, :], 144, [[-1, 16], [-16, 9]], 0, 1, ("IZ", 0, 144))
+    pool(T.X0[:, :], P, [[1, P]], OWN[0], 0, ("X0", 0, P), True)
+
+    cp(("SU", 0, P), ("SI", 0, P))
+    cp(("SW0", 0, P), ("SI", 0, P))
+    ts(("IK2", 0, 128), ("IK", 0, 128), 4, None, ALU.arith_shift_right)
+    ts(("E", 0, 128), ("IK2", 0, 128), 0.0, None, ALU.is_equal)
+    ts(("ID", 0, 128), ("II", 0, 128), 0.0, None, ALU.is_equal)
+    op("v", 64 + OVH, lambda e: V.tensor_scalar(T.GM[:, :], T.E[:, 0:128:16], 1.0 / 256, None, ALU.mult),
+       [("E", 0, 128)], [("GM", 0, 8)])
+    for a in range(8):
+        if a < 4:
+            fn = lambda e, a=a: V.tensor_scalar(T.MB[:, :, a, :], T.MT[:, :], T.GM[:, a:a + 1], None, ALU.mult)
+        else:
+            fn = lambda e, a=a: S.activation(T.MB[:, :, a, :], T.MT[:, :], ACT.Identity, scale=T.GM[:, a:a + 1])
+        op("v" if a < 4 else "a", (128 if a < 4 else 256) + OVH, fn, [("MT", 0, 256), ("GM", 0, 8)], [("MB", a, a + 1)])
+    ts(("IP", 2, 3), ("IP", 0, 1), 15, None, ALU.bitwise_and)
+    ts(("IP", 4, 5), ("IP", 0, 1), 1, None, ALU.bitwise_and)
+    cp(("COL", 0, 1), ("IP", 2, 3))
+    cp(("COL", 1, 2), ("IP", 4, 5))
+    ts(("COL", 2, 3), ("COL", 1, 2), 257.0, -1.0, ALU.mult, ALU.add)
+    ts(("COL", 3, 4), ("COL", 1, 2), -1536.0, 1535.5, ALU.mult, ALU.add)
+    ts(("COL", 4, 5), ("COL", 1, 2), 1792.0, -0.5, ALU.mult, ALU.add)
+    ts(("COL", 5, 6), ("COL", 0, 1), 0.0, 64.0, ALU.is_equal, ALU.mult)
+    ts(("COL", 6, 7), ("COL", 0, 1), 1.0, None, ALU.is_equal)
+    tt(("COL", 7, 8), ("COL", 5, 6), ("COL", 6, 7), ALU.add)
+    ts(("IL", 0, 64), ("IM", 0, 64), ("COL", 0, 1), None, ALU.add)
+    fill(("ZB", 0, 144), 0.0)
+    op("v", 64 + OVH, lambda e: V.tensor_copy(T.ZB[:, 15:143:16], T.E[:, 0:128:16]), [("E", 0, 128)], [("ZB", 0, 144)])
+    ts(("ZK", 0, 144), ("ZB", 0, 144), 65536.0, None, ALU.mult)
+    ts(("ZH", 0, 144), ("ZB", 0, 144), ("COL", 7, 8), None, ALU.mult)
+    fill(("ZR", 0, 2304), 0.0)
+    op("v", 144 + OVH, lambda e: V.tensor_scalar(T.ZR[:, 15:2304:16], T.IZ[:, :], 0.0, None, ALU.is_equal),
+       [("IZ", 0, 144)], [("ZR", 0, 2304)])
+    cp(("Z32", 0, 144), ("ZR", 5 * 144, 6 * 144))
+    cp(("Z32", 144, 288), ("ZR", 11 * 144, 12 * 144))
+    ts(("PEN", 0, 128), ("E", 0, 128), -4096.0, None, ALU.mult)
+    ts(("NL", 0, 128), ("ID", 0, 128), 4096.0, None, ALU.mult)
+    tt(("LM", 0, 128), ("NL", 0, 128), ("E", 0, 128), ALU.max)
+    ts(("NL", 0, 128), ("LM", 0, 128), -1.0, None, ALU.mult)
+    fill(("CH", 0, 512), -1152.0)
+    cp(("I16", 0, 128), ("ID", 0, 128))
+    fill(("CN", 0, 32), 0.0)
+    fill(("CN", 32, 96), -983040.0)
+    fill(("CB1", 0, 256), float(P + GH))
+    fill(("CB2", 0, 256), float(P + 2 * GH))
+    ts(("S16", 0, P), ("SU", 0, P), float(-OFF16), None, ALU.add)
+    ts(("TM", 0, 256), ("SI", 0, 256), ("COL", 2, 3), None, ALU.is_lt)
+    ts(("TV", 0, 256), ("SI", 0, 256), float(P), None, ALU.add)
+    tt(("TS0", 0, 256), ("TM", 0, 256), ("TV", 0, 256), ALU.mult)
+    send_tuples(0)
+    pool(T.HL[0:64, :], 2304, [[1, 36], [0, 64]], 0, 0, ("HL", 0, 2304, 0), True)
+    pool(T.HL[64:128, :], 2304, [[0, 36], [1, 64]], 0, 0, ("HL", 0, 2304, 1), True)
+    pool(T.X1[:, :], P, [[1, P]], OWN[1], 0, ("X1", 0, P), True)
+    pool(T.X2[:, :], P, [[1, P]], OWN[2], 0, ("X2", 0, P), True)
+    for h in range(2):
+        dma(T.FT[h:128:2, 0:2304], T.HL[64 * h:64 * h + 64, :], [("HL", 0, 2304, h)], [("FT", 0, 2304, h)])
+    dma(T.DTa[:, P:2304], T.FT[:, P:2304], [("FT", P, 2304)], [("DTa", P, 2304)])
+    dma(T.DTb[:, P:2304], T.FT[:, P:2304], [("FT", P, 2304)], [("DTb", P, 2304)])
+    dma(T.FT[:, 2304:3328], T.FT[:, 0:P], [("FT", 0, P)], [("FT", 2304, 3328)])
+    dma(T.FT[:, 3328:5632], T.FT[:, 0:2304], [("FT", 0, 2304)], [("FT", 3328, 5632)])
+
+    def guests(src):
+        tolist("P7", 0, "ZB", 0, src)
+        tt(("GI", 0, 64), ("P7", 0, 64), ("IL", 0, 64), ALU.add)
+        ts(("GJ", 0, 64), ("GI", 0, 64), GH - 1, None, ALU.bitwise_and)
+        cp(("GL", 0, 64), ("GJ", 0, 64))
+
+    def klist(t, ks, sw):
+        wide = t == 2 and ks[0] == 1
+        for k in ks:
+            if wide:
+                tolist("P4", 64 * k, "Z32", 144 * (k // 2), (sw, 0, P), slow=4)
+            else:
+                tolist("P4", 64 * k, "ZR", 144 * (3 * k + t), ("S16", 0, P))
+            off = 0.0 if wide else float(OFF16)
+            ts(("KL", 64 * k, 64 * k + 64), ("P4", 64 * k, 64 * k + 64), off, None, ALU.add)
+            act(("KY", 64 * k, 64 * k + 64), ("P4", 64 * k, 64 * k + 64), ACT.Identity, off + 8192.0 * (5 - k))
+
+    def compose(buf, t):
+        if t == 2:
+            gat2((buf, 2304, 3328), (buf, 3328, 5632), ("LB", 0, 64))
+        if t >= 1:
+            gat2((buf, 0, P), (buf, P, 3328), ("LA", 0, 64))
+
+    def one_round(t):
+        W, sw, sn, X, TG = "W%d" % t, "SW%d" % (t % 2), "SW%d" % ((t + 1) % 2), "X%d" % t, "TG%d" % t
+        par = (t + 1) % 2
+        own = OWN[t]
+        vb, v0 = ("W%d" % (t + 1), OWN[t + 1]) if t + 1 < RO else ("VN", 0)
+        dma(T[X][1 - par:128:2, :], T[sw][1 - par:128:2, 0:P], [(sw, 0, P)], [(X, 0, P)])
+        dma(T.UW[:, P:2304], T[W][:, P:2304], [(W, P, 2304)], [("UW", P, 2304)])
+        if t == 2:
+            dma(T.UW[:, 4352:5632], T[W][:, P:2304], [(W, P, 2304)], [("UW", 4352, 5632)])
+
+        def cands(b):
+            gtt((sw, P + 512 * b, P + 512 * b + 512), (TG, 0, 256), ("GL", 32 * b, 32 * b + 32), (X, 512 * b, 512 * b + 512),
+                ALU.max if t == 0 else ALU.min)
+            for h in range(2):
+                pp = par if h == 0 else 1 - par
+                lo = P + 512 * b + 256 * h
+                dma(T.C2f[pp:128:2, 256 * b:256 * b + 256], T[sw][par:128:2, lo:lo + 256], [(sw, lo, lo + 256)],
+                    [("C2f", 256 * b, 256 * b + 256, pp)])
+            cp(("C2u", 256 * b, 256 * b + 256), ("C2f", 256 * b, 256 * b + 256))
+
+        def old(c0, half, bank, stop=False):
+            mm([(c0 % 512, c0 % 512 + ACH, T.MB[:, o, :, :], T.GA[:, 16 * c0 + o:16 * (c0 + ACH):16], False)
+                for o in range(half, 16, 2)], [("GA", 16 * c0, 16 * (c0 + ACH)), ("MB", 0, 8)], bank, stop=stop)
+
+        def kept(b, lo, hi):
+            for c0 in range(512 * b + lo, 512 * b + hi, ACH):
+                gat(("GA", 16 * c0, 16 * (c0 + ACH)), (W, 0, WIN[t]), ("SU", c0, c0 + ACH))
+                old(c0, 1 - par, "A%d" % b)
+                old(c0, par, "A%d" % b, c0 % 512 + ACH == 512)
+                old(c0, 1 - par, "B%d" % b)
+
+        def worth(b):
+            ts(("AI", 512 * b, 512 * b + 512), ("A%d" % b, 0, 512), 255.25, -255.0 / 512, ALU.min, ALU.add)
+
+        def choose(b):
+            bank = "B%d" % b
+            for c0 in range(256 * b, 256 * b + 256, BCH):
+                gat(("GB", 16 * c0, 16 * (c0 + BCH)), (W, 0, WIN[t]), ("C2u", c0, c0 + BCH))
+                m0 = c0 % 256
+                it = []
+                for s in range(16):
+                    h = 0 if s % 2 == par else 1
+                    o = s if h == 0 else s ^ 1
+                    it.append((256 * h + m0, 256 * h + m0 + BCH, T.MB[:, o, :, :], T.GB[:, 16 * c0 + s:16 * (c0 + BCH):16],
+                               False))
+                mm(it, [("GB", 16 * c0, 16 * (c0 + BCH)), ("MB", 0, 8)], bank, stop=m0 + BCH == 256)
+            lo, hi = 512 * b, 512 * b + 512
+            tt(("LT", lo, hi), (bank, 0, 512), ("AI", lo, hi), ALU.is_lt)
+            ts(("B16", lo, hi), (bank, 0, 512), 255.25, 1152 - 255.0 / 512, ALU.min, ALU.add)
+            bank = "A%d" % b
+            mm([(0, 512, T.ID[:, :], T.CH[:, :], True), (0, 512, T.PEN[:, :], T.LT[:, lo:hi], False)],
+               [("PEN", 0, 128), ("LT", lo, hi), ("ID", 0, 128), ("CH", 0, 512)], bank, stop=False)
+            mm([(0, 512, T.I16[:, :], T.B16[:, lo:hi], False)], [("I16", 0, 128), ("B16", lo, hi)], bank)
+            tt(("UW", own + lo, own + hi), (bank, 0, 512), ("AI", lo, hi), ALU.max)
+            if b == 0:
+                dma(T[vb][:, v0:v0 + 512], T.UW[:, own:own + 512], [("UW", own, own + 512)], [(vb, v0, v0 + 512)])
+            else:
+                cp((vb, v0 + lo, v0 + hi), ("UW", own + lo, own + hi))
+            if b == 0 and t + 1 < RO:
+                send_values(t + 1, ("UW", own, own + GH))
+            x, y = 32 * b, 32 * b + 32
+            tolist("P6", x, "ZB", 0, ("LT", lo, hi))
+            ts(("OA", x, y), ("P6", x, y), 0.0, float(P), ALU.is_equal, ALU.mult)
+            tt(("OB", x, y), ("OA", x, y), ("IL", x, y), ALU.add)
+            cp(("OL", x, y), ("OB", x, y))
+            gat((sn, lo, hi), (sw, 0, 2 * P), ("OL", x, y))
+            cp(("SU", lo, hi), (sn, lo, hi))
+            if t + 1 < RO:
+                ts(("S16", lo, hi), ("SU", lo, hi), float(-OFF16), None, ALU.add)
+            if t + 1 < RO and b == 0:
+                for h in range(2):
+                    pp = (1 - par) if h == 0 else par
+                    dma(T.SNf[pp:128:2, :], T[sn][1 - par:128:2, 128 * h:128 * h + 128], [(sn, 128 * h, 128 * h + 128)],
+                        [("SNf", 0, 128, pp)])
+                cp(("SNu", 0, 128), ("SNf", 0, 128))
+
+        for b in range(2):
+            for bank in ("A%d" % b, "B%d" % b):
+                mm([(0, 512, T.ID[:, :], T.RW[:, 512 * b:512 * b + 512], True)],
+                   [("ID", 0, 128), ("RW", 512 * b, 512 * b + 512)], bank, stop=False)
+        kept(0, 0, 512)
+        worth(0)
+        cands(0)
+        cands(1)
+        kept(1, 0, 256)
+        choose(0)
+        kept(1, 256, 512)
+        worth(1)
+        choose(1)
+        vn = ("UW", own, own + P)
+        if t == 1:
+            dma(T.W2[:, 4352:5632], T.W2[:, P:2304], [("W2", P, 2304)], [("W2", 4352, 5632)])
+        if t + 1 == RO:
+            dma(T.yv[:, :], ap(vn), [vn], [])
+        compose("UW", t)
+        klist(t, [1, 3], sn)
+        act(("AC", 0, 64), ("IL", 0, 64), ACT.Identity, float(own))
+        uw = ("UW", 0, WIN[t])
+        for j, k in enumerate(KORD):
+            df, bank, col, way = "DF%d" % k, ("P5" if j % 2 == 0 else "P6"), 64 * (k + 1), WAYS[k]
+            for b in range(2):
+                lo, hi, bk = 512 * b, 512 * b + 512, ("A%d" if k == 0 else "B%d") % b
+                kl = ("KL", 64 * k + 32 * b, 64 * k + 32 * b + 32)
+                if way[b] == "a":
+                    sg = "SG%d" % (j % 2)
+                    gat((sg, lo, hi), uw, kl, eng="a")
+                    mm([(0, 512, T.NL[:, :], T.UW[:, own + lo:own + hi], True),
+                        (0, 512, T.LM[:, :], T[sg][:, lo:hi], False)],
+                       [("NL", 0, 128), ("LM", 0, 128), ("UW", own + lo, own + hi), (sg, lo, hi)], bk)
+                    act((df, lo, hi), (bk, 0, 512), ACT.Sign, -0.5)
+                elif way == "vv" and b == 0:
+                    gtt((df, 0, P), uw, ("KL", 64 * k, 64 * k + 64), (vb, v0, v0 + P), ALU.subtract)
+                    ts((df, 0, P), (df, 0, P), 16.0, 1.0, ALU.mult, ALU.min)
+                elif way != "vv":
+                    gtt((df, lo, hi), uw, kl, (vb, v0 + lo, v0 + hi), ALU.subtract)
+                    ts((df, lo, hi), (df, lo, hi), 16.0, 1.0, ALU.mult, ALU.min)
+            tolist(bank, col, "ZK", 0, (df, 0, P), tail={"aa": ("CN", 32, 96), "va": ("CN", 0, 64), "vv": None}[way])
+            tt(("ZZ", 64 * k, 64 * k + 64), (bank, col, col + 64), ("KY", 64 * k, 64 * k + 64), ALU.min)
+            nxt = ("AJ", 0, 64) if j == 4 else ("AC", 64 * j + 64, 64 * j + 128)
+            tt(nxt, ("AC", 64 * j, 64 * j + 64), ("ZZ", 64 * k, 64 * k + 64), ALU.max)
+        ts(("AK", 0, 64), ("AJ", 0, 64), 8191, None, ALU.bitwise_and)
+        cp(("DR", 0, 64), ("AK", 0, 64))
+        gat2(("DTa", 0, P), ("FT", 0, WIN[t]), ("DR", 0, 64))
+        d1 = ("DR", 0, 64)
+        if t > 0:
+            tolist("P6", 448, "ZH", 0, ("DTa", 0, P))
+            d1 = ("D1", 0, 64)
+            cp(d1, ("P6", 448, 512))
+        if t + 1 < RO:
+            guests(vn)
+            klist(t + 1, [0, 2, 4], None)
+        gat2(("DTb", 0, P), ("DTa", 0, 2304), d1)
+        gat2(("DTa", 0, P), ("DTb", 0, 2304), d1)
+        gat2(("FT", own, own + P), ("DTa", 0, 2304), d1)
+        if t + 1 < RO:
+            tolist("P5", 448, "ZH", 0, ("FT", own, own + P))
+            if t == 0:
+                ts(("LC", 0, 64), ("P5", 448, 512), float(P), 2304.0, ALU.is_lt, ALU.mult)
+                tt(("LD", 0, 64), ("P5", 448, 512), ("LC", 0, 64), ALU.add)
+                ts(("LA", 0, 64), ("LD", 0, 64), float(-P), None, ALU.add)
+            else:
+                cp(("LB", 0, 64), ("P5", 448, 512))
+                gat2(("FT", 0, P), ("FT", P, 3328), ("LA", 0, 64))
+            for h in range(2):
+                gat(("GS", P * h, P * h + P), ("FT", 0, WIN[t]), ("SNu", 64 * h, 64 * h + 64))
+            cb = "CB%d" % (t + 1)
+            it = [(64, 320, T.ID[:, :], T[cb][:, :], True)]
+            for s in range(16):
+                h = 0 if s % 2 == 1 - par else 1
+                o = s if h == 0 else s ^ 1
+                it.append((64 + 128 * h, 192 + 128 * h, T.ZH[:, 15 - o:143 - o], T.GS[:, s:2048:16], False))
+            mm(it, [("ID", 0, 128), (cb, 0, 256), ("ZH", 0, 144), ("GS", 0, 2048)], "P7")
+            ts(("TM", 0, 256), ("P7", 64, 320), ("COL", 3 + t, 4 + t), 8192.0, ALU.is_ge, ALU.mult)
+            tt(("TS%d" % (t + 1), 0, 256), ("P7", 64, 320), ("TM", 0, 256), ALU.add)
+            send_tuples(t + 1)
+            compose("W%d" % (t + 1), t + 1)
+
+    guests(("W0", 0, P))
+    klist(0, [0, 2, 4], None)
+    for t in range(RO):
+        one_round(t)
+    compose("FT", 2)
+    for j, (c0, w) in enumerate(LAST):
+        bank = PSUM[j % 4]
+        gat(("GA", 16 * c0, 16 * (c0 + w)), ("FT", 0, WIN[2]), ("SU", c0, c0 + w))
+        mm([(0, w, T.ZH[:, 15 - o:143 - o], T.GA[:, 16 * c0 + o:16 * (c0 + w):16], o == 0) for o in range(16)],
+           [("ZH", 0, 144), ("GA", 16 * c0, 16 * (c0 + w))], bank)
+        move(("YS", c0, c0 + w), (bank, 0, w))
+        if j % 2 == 1:
+            dma(T.ys[:, c0 - w:c0 + w], T.YS[:, c0 - w:c0 + w], [("YS", c0 - w, c0 + w)], [])
+    return ops
+
+
+def order(ops):
+    n = len(ops)
+    pre = [set() for _ in range(n)]
+    seen = {}
+    for i, o in enumerate(ops):
+        if o["after"] is not None:
+            pre[i].add(o["after"])
+        for x, wr in [(x, False) for x in o["r"]] + [(x, True) for x in o["w"]]:
+            lst = seen.setdefault(x[0], [])
+            for j, y, wy in (lst[-1:] if x[0] in PSUM else lst):
+                if x[0] in PSUM or ((wr or wy) and _conf(x, y)):
+                    pre[i].add(j)
+        for x in o["r"]:
+            seen[x[0]].append((i, x, False))
+        for x in o["w"]:
+            seen[x[0]].append((i, x, True))
+    pre = [sorted(x) for x in pre]
+    cost = [o["cost"] for o in ops]
+    hold = [{"c": o["cost"], "d": 100.0, "r": 600.0, "x": 0.0}[o["kind"]] for o in ops]
+    near = [[(j, 0.0 if ops[i]["eng"] == "p" and ops[j]["eng"] == "p" else LAT) for j in pre[i]] for i in range(n)]
+
+    def place(key, pick):
+        key = list(key)
+        for i in range(n):
+            for j in pre[i]:
+                if key[j] >= key[i]:
+                    key[i] = key[j] + 1e-4
+        busy = {e: [] for e in "vapgsx"}
+        start, end, why = [0.0] * n, [0.0] * n, [-1] * n
+        for i in sorted(range(n), key=lambda i: key[i]):
+            s, w = 0.0, -1
+            for j, d in near[i]:
+                if end[j] + d > s:
+                    s, w = end[j] + d, j
+            q = busy[pick[i]]
+            k = len(q)
+            while k and q[k - 1][1] > s:
+                k -= 1
+            while k < len(q) and s + hold[i] > q[k][0]:
+                if q[k][1] > s:
+                    s, w = q[k][1], q[k][2]
+                k += 1
+            q.insert(k, (s, s + hold[i], i))
+            start[i], end[i], why[i] = s, s + cost[i], w
+        return start, end, why
+
+    pick = [o["eng"][-1] if i % 5 < 3 else o["eng"][0] for i, o in enumerate(ops)]
+    res = place(range(n), pick)
+    best = (res, pick)
+    x = SEED
+    for it in range(TRIES):
+        i = max(range(n), key=lambda i: res[1][i])
+        pairs = []
+        while res[2][i] >= 0:
+            j = res[2][i]
+            if j not in pre[i]:
+                pairs.append((j, i))
+            i = j
+        x = (x * 1103515245 + 12345) % 2147483648
+        j, i = pairs[(x >> 8) % len(pairs)]
+        x = (x * 1103515245 + 12345) % 2147483648
+        how = (x >> 12) % 5
+        key, p2 = list(res[0]), list(pick)
+        if how == 0 and len(ops[i]["eng"]) > 1:
+            p2[i] = "a" if p2[i] == "v" else "v"
+        elif how == 1 and len(ops[j]["eng"]) > 1:
+            p2[j] = "a" if p2[j] == "v" else "v"
+        elif how == 2:
+            key[j] = key[i] + (x >> 16) % 2000
+        else:
+            key[i] = key[j] - 1 - ((x >> 16) % 3000 if how == 3 else 0)
+            stack = [i]
+            while stack:
+                a = stack.pop()
+                for b in pre[a]:
+                    if key[b] >= key[a]:
+                        key[b] = key[a] - 1e-3
+                        stack.append(b)
+        r2 = place(key, p2)
+        if max(r2[1]) <= max(res[1]) + SLACK * (1 - it / TRIES):
+            res, pick = r2, p2
+            if max(res[1]) < max(best[0][1]):
+                best = (res, pick)
+    return pre, best[0][0], best[0][1], best[1]
+
+
+def rank_program(g, core, T, topo):
+    if T.rank_of(core) is None:
+        return
+    ops = build(g, core, T, topo)
+    if "plan" not in PLAN:
+        PLAN["plan"] = order(ops)
+    pre, start, end, eng = PLAN["plan"]
+    seq = sorted(range(len(ops)), key=lambda i: (start[i], i))
+    place = {i: k for k, i in enumerate(seq)}
+    queue = {"v": g.vector, "a": g.scalar, "p": g.tensor, "g": g, "s": g.sync}
+    need, marked, known = {}, set(), {e: {} for e in queue}
+    for i in seq:
+        if ops[i]["kind"] == "x":
+            continue
+        e, lst, last = eng[i], [], {}
+        for j in pre[i]:
+            if ops[j]["kind"] == "c":
+                if not (e == "p" and eng[j] == "p") and place[j] > last.get(eng[j], (-1, 0))[0]:
+                    last[eng[j]] = (place[j], j)
+            elif j not in known[e]:
+                known[e][j] = 1
+                lst.append(j)
+        for f, (pl, j) in last.items():
+            if known[e].get(f, -1) < pl:
+                known[e][f] = pl
+                marked.add(j)
+                lst.append(j)
+        need[i] = lst
+    count, total, nd = {}, {}, 0
+    for i in seq:
+        o = ops[i]
+        if o["kind"] == "c":
+            if i in marked:
+                s = "c" + eng[i]
+                total[s] = total.get(s, 0) + 1
+                count[i] = (s, total[s])
+        else:
+            if o["kind"] == "x":
+                s = o["sem"]
+            else:
+                s = "d%d" % nd
+                nd += 1
+            total[s] = o["inc"]
+            count[i] = (s, o["inc"])
+    for i in seq:
+        o = ops[i]
+        if o["kind"] == "x":
+            continue
+        for j in need[i]:
+            queue[eng[i]].wait_ge(T.sem[count[j][0]], count[j][1])
+        if o["kind"] == "r":
+            o["fn"](eng[i], T.sem[count[i][0]])
+        else:
+            ins = o["fn"](eng[i])
+            if i in count:
+                ins.then_inc(T.sem[count[i][0]], o["inc"])
+    for s in sorted(total):
+        g.sync.wait_ge(T.sem[s], total[s])

@@ -1,24 +1,28 @@
+import numpy as np
 from concourse.bass import DstId, RemoteDMATransfer
 from concourse.mybir import AluOpType, ActivationFunctionType
 
 ALU = AluOpType
 ACT = ActivationFunctionType
 P, GH, NR, RO = 1024, 256, 6, 3
-OWN = [0, 2304, 3328]
-WIN = [2304, 3328, 4352]
-OFF16 = 1664
+B2, B0, GO, B1, END = 0, 1024, 2048, 3328, 4352
+OWN = [B0, B1, B2]
+BASE = [B0, B0, B2]
+STOP = [B1, END, END]
+OFF = [1280, 1024]
+BIG = 8192.0
 
 bf, f32, i32, u16, f16 = "bfloat16", "float32", "int32", "uint16", "float16"
 SCRATCH = {"MB": ("sbuf", [128, 16, 8, 16], bf)}
 for _dt, _list in (
-        (bf, "W0 2304 W1 3328 W2 5632 UW 5632 FT 5632 DTa 2304 DTb 2304 HL 2304 GA 16384 GB 8192 GS 2048 RW 1024 MT 256 LT 1024 "
-             "DF0 1024 DF1 1024 DF2 1024 DF3 1024 DF4 1024 SG0 1024 SG1 1024 E 128 ID 128 LM 128 NL 128 PEN 128 ZB 144 ZK 144 ZH 144 "
-             "CH 512 CN 96 CB1 256 CB2 256 VN 1024"),
-        (f32, "SW0 2048 SW1 2048 X0 1024 X1 1024 X2 1024 TG0 256 TG1 256 TG2 256 TS0 256 TS1 256 TS2 256 TM 256 TV 256 C2f 512 "
-              "SNf 128 YS 1024 COL 16 GM 8 Z32 288 IL 64 OA 64 OB 64 KY 320 ZZ 320 AC 384 LC 64 LD 64"),
-        (i32, "SI 1024 AI 1024 IK 128 IK2 128 II 128 IZ 144 IM 64 IP 8 GI 64 GJ 64 AJ 64 AK 64"),
-        (u16, "SU 1024 C2u 512 SNu 128 GL 64 OL 64 KL 320 DR 64 D1 64 LA 64 LB 64"),
-        (f16, "S16 1024 ZR 2304 B16 1024 I16 128")):
+        (bf, "GX 8192 GY 8192 GZ 8192 GS 2048 W0 3328 W1 4352 W2 4352 UW 4352 FT 4352 DTa 2304 DTb 2304 HL 2304 RW 1024 VN 1024 MT 256 LT 1024 "
+             "DF0 1024 DF1 1024 DF2 1024 DF3 1024 DF4 1024 SG0 1024 SG1 1024 E 128 ID 128 LM 128 NL 128 PEN 128 EN 128 "
+             "ZB 144 ZK 144 ZH 144 ZA 144 ZC 144 ZP 144 ZM 144 EM 144 EP 144 CH 512 CN 96"),
+        (f32, "F 4352 FO 6144 X0 1024 X1 1024 X2 1024 TG0 256 TG1 256 TG2 256 TS0 256 TS1 256 TS2 256 TM 256 "
+              "COL 16 OH 4 GM 8 IL 64 KY 320 ZZ 320 AC 384"),
+        (i32, "SI 1024 AI 1024 IK 128 IK2 128 II 144 IZ 72 IM 64 IP 8 IO 4 GI 64 GJ 64 AJ 64 AK 64"),
+        (u16, "HU0 512 HU1 512 CU 512 GL 64 KL 320 DR 64 D1 64 D2 64 LA 64 LB 64 FL 1024"),
+        (f16, "S16 1024 ZR 1152 I16 128 R0 144 R1 144 H0 512 H1 512 TT 512 CG 1024 B16 1024")):
     _w = _list.split()
     for _k in range(0, len(_w), 2):
         SCRATCH[_w[_k]] = ("sbuf", [128, int(_w[_k + 1])], _dt)
@@ -26,14 +30,18 @@ PSUM = ("A0", "A1", "B0", "B1", "P4", "P5", "P6", "P7")
 for _k in PSUM:
     SCRATCH[_k] = ("psum", [128, 512], f32)
 SEMAPHORES = (["cv", "ca", "cp", "cg"] + ["arV%d" % t for t in range(RO)] + ["arT%d" % t for t in range(RO)]
-              + ["d%d" % k for k in range(64)])
+              + ["d%d" % k for k in range(80)])
 
 CG, CPE, LAT, OVH, CDMA, CREM = 1.55, 0.55, 150.0, 70.0, 2400.0, 4500.0
-TRIES, SEED, SLACK = 25000, 3, 250.0
-ACH, BCH = 64, 64
-LAST = [(128 * j, 128) for j in range(6)] + [(768 + 64 * j, 64) for j in range(4)]
+TRIES, SEED, SLACK, NOISE = 12000, 3, 400.0, 3000.0
+CHUNKS = [(0, 384), (384, 896), (896, 1024)]
+BANKS = [("A0", "B0"), ("A1", "B1"), ("P6", "P7")]
+CANDS = [(0, 512), (512, 1024)]
+GCH, XCH = 64, 64
 WAYS = ["aa", "vv", "aa", "vv", "va"]
-KORD = [4, 0, 1, 2, 3]
+KORD = [4, 0, 2, 1, 3]
+SLOTS = 6
+BIAS = 300.0
 PLAN = {}
 
 
@@ -49,9 +57,9 @@ def build(g, core, T, topo):
     def reg(x):
         return x if len(x) == 4 else (x[0], x[1], x[2], None)
 
-    def op(eng, cost, fn, r, w, kind="c", after=None, sem=None, inc=1):
+    def op(eng, cost, fn, r, w, kind="c", after=None, sem=None, inc=1, cls=None):
         ops.append({"eng": eng, "cost": cost, "fn": fn, "r": [reg(x) for x in r], "w": [reg(x) for x in w],
-                    "kind": kind, "after": after, "sem": sem, "inc": inc})
+                    "kind": kind, "after": after, "sem": sem, "inc": inc, "cls": cls})
         return len(ops) - 1
 
     def ap(x):
@@ -64,11 +72,12 @@ def build(g, core, T, topo):
         n = in_[2] - in_[1]
         c = max(64, n * (0.5 if two(out) and two(in_) else 1.0)) + OVH
         a1 = ap(s1) if isinstance(s1, tuple) else s1
+        a2 = ap(s2) if isinstance(s2, tuple) else s2
         if o1 is None:
             fn = lambda e: V.tensor_scalar(ap(out), ap(in_), a1, None, o0)
         else:
-            fn = lambda e: V.tensor_scalar(ap(out), ap(in_), a1, s2, o0, o1)
-        return op("v", c, fn, [in_] + ([s1] if isinstance(s1, tuple) else []), [out])
+            fn = lambda e: V.tensor_scalar(ap(out), ap(in_), a1, a2, o0, o1)
+        return op("v", c, fn, [in_] + [x for x in (s1, s2) if isinstance(x, tuple)], [out])
 
     def cp(out, in_):
         n = in_[2] - in_[1]
@@ -81,13 +90,17 @@ def build(g, core, T, topo):
         return op("v", c, lambda e: V.tensor_tensor(ap(out), ap(a), ap(b), o), [a, b], [out])
 
     def act(out, in_, func, bias):
-        return op("a", in_[2] - in_[1] + OVH, lambda e: S.activation(ap(out), ap(in_), func, bias=bias), [in_], [out])
+        return op("a", max(64, in_[2] - in_[1]) + OVH, lambda e: S.activation(ap(out), ap(in_), func, bias=bias), [in_], [out])
 
-    def move(out, in_):
+    def scale(out, in_, col):
+        return op("a", in_[2] - in_[1] + OVH, lambda e: S.activation(ap(out), ap(in_), ACT.Identity, scale=ap(col)),
+                  [in_, col], [out])
+
+    def move(out, in_, add=0.0):
         def fn(e):
             if e == "v":
-                return V.tensor_copy(ap(out), ap(in_))
-            return S.activation(ap(out), ap(in_), ACT.Copy)
+                return V.tensor_scalar(ap(out), ap(in_), add, None, ALU.add)
+            return S.activation(ap(out), ap(in_), ACT.Identity, bias=add)
         return op("va", in_[2] - in_[1] + OVH, fn, [in_], [out])
 
     def gat(out, win, off, eng="va"):
@@ -96,7 +109,7 @@ def build(g, core, T, topo):
             if e == "v":
                 return V.tensor_copy(ap(out), src)
             return S.activation(ap(out), src, ACT.Copy)
-        return op(eng, (out[2] - out[1]) * CG + OVH, fn, [win, off], [out])
+        return op(eng, (out[2] - out[1]) * CG + OVH, fn, [win, off], [out], cls="g")
 
     def gat2(out, win, off):
         for h in range(2):
@@ -104,30 +117,46 @@ def build(g, core, T, topo):
 
     def gtt(out, win, off, b, o):
         return op("v", (out[2] - out[1]) * CG + OVH,
-                  lambda e: V.tensor_tensor(ap(out), ap(win).indirect(ap(off)), ap(b), o), [win, off, b], [out])
+                  lambda e: V.tensor_tensor(ap(out), ap(win).indirect(ap(off)), ap(b), o), [win, off, b], [out], cls="g")
 
-    def mm(items, r, bank, slow=1, stop=True):
+    def mm(items, r, bank, step=1):
+        me = len(ops)
+
         def fn(e):
             last = None
             for k, (lo, hi, l, x, st) in enumerate(items):
-                last = PE.matmul(T[bank][:, lo:hi], l, x, st, stop and k == len(items) - 1)
+                last = PE.matmul(T[bank][:, lo:hi:step], l, x, st, ops[me]["stop"] and k == len(items) - 1)
             return last
-        c = sum(max(64, it[1] - it[0]) for it in items) * CPE * slow + OVH
-        return op("p", c, fn, r, [(bank, min(it[0] for it in items), max(it[1] for it in items))])
+        c = sum(max(64, (it[1] - it[0] + step - 1) // step) for it in items) * CPE + OVH
+        return op("p", c, fn, r, [(bank, min(it[0] for it in items), max(it[1] for it in items))],
+                  cls=None if items[0][4] else "add")
 
-    def tolist(bank, lo, z, z0, src, tail=None, slow=1):
+    def tolist(bank, lo, z, src, tail=None):
         n = src[2] - src[1]
-        it = [(lo, lo + n // 16, T[z][:, z0 + 15 - q:z0 + 143 - q], T[src[0]][:, src[1] + q:src[2]:16], q == 0)
+        it = [(lo, lo + n // 16, T[z][:, 15 - q:143 - q], T[src[0]][:, src[1] + q:src[2]:16], q == 0)
               for q in range(16)]
-        r = [src, (z, z0, z0 + 144)]
+        r = [src, (z, 0, 144)]
         if tail is not None:
             it.append((lo, lo + n // 16, T.ID[:, :], ap(tail), False))
             r += [tail, ("ID", 0, 128)]
-        return mm(it, r, bank, slow)
+        return mm(it, r, bank)
+
+    def rowlist(bank, lo, o):
+        h = "H%d" % (o % 2)
+        z0 = 144 * (o // 2) + 14
+        it = [(lo, lo + 64, T.ZR[:, z0 - 2 * u:z0 - 2 * u + 128], T[h][:, u:512:8], u == 0) for u in range(8)]
+        return mm(it, [(h, 0, 512), ("ZR", 0, 1152)], bank)
+
+    def fold(e, src, n0, n1, lo, start):
+        r = T["R%d" % e]
+        return [(lo, lo + (n1 - n0) // 2, r[:, 1 - h:129 - h], T[src][:, n0 + h:n1:2], start and h == 0) for h in range(2)]
 
     def dma(out, in_, r, w, eng="s"):
         q = {"s": g.sync, "a": g.scalar}[eng]
         return op(eng, CDMA, lambda e: q.dma_start(out, in_), r, w, kind="d", inc=16)
+
+    def copy(out, in_):
+        return dma(ap(out), ap(in_), [in_], [out])
 
     def pool(out, n, pattern, base, cm, w, small=False):
         if small:
@@ -158,211 +187,211 @@ def build(g, core, T, topo):
         op("x", 1, None, [], [land], kind="x", after=k, sem=sem, inc=ne * len(dests))
 
     def send_values(t, src):
-        dests = [(T.cores[(rank - d) % NR], T["W%d" % t][:, P + (d - 1) * GH:P + d * GH]) for d in range(1, NR)]
-        send(src, dests, "arV%d" % t, ("W%d" % t, P, 2304), CREM + 2500)
+        dests = [(T.cores[(rank - d) % NR], T["W%d" % t][:, GO + (d - 1) * GH:GO + d * GH]) for d in range(1, NR)]
+        send(src, dests, "arV%d" % t, ("W%d" % t, GO, B1), CREM + 2500)
 
     def send_tuples(t):
         send(("TS%d" % t, 0, 256), [(T.cores[(rank - t - 1) % NR], T["TG%d" % t][:, :])], "arT%d" % t,
              ("TG%d" % t, 0, 256), CREM)
 
-    dma(T.W0[:, 0:GH], T.v0[:, 0:GH], [], [("W0", 0, GH)])
-    dma(T.SI[:, :], T.succ[:, :], [], [("SI", 0, P)], eng="a")
-    dma(T.W0[:, GH:P], T.v0[:, GH:P], [], [("W0", GH, P)])
+    def col(k):
+        return ("COL", k, k + 1)
+
+    dma(T.W0[:, B0:B0 + GH], T.v0[:, 0:GH], [], [("W0", B0, B0 + GH)])
+    dma(T.SI[:, 0:GH], T.succ[:, 0:GH], [], [("SI", 0, GH)], eng="a")
+    dma(T.W0[:, B0 + GH:GO], T.v0[:, GH:P], [], [("W0", B0 + GH, GO)])
+    dma(T.SI[:, GH:P], T.succ[:, GH:P], [], [("SI", GH, P)], eng="a")
     dma(T.MT[:, :], T.mat[:, :], [], [("MT", 0, 256)])
     dma(T.RW[:, :], T.rew[:, :], [], [("RW", 0, P)], eng="a")
-    pool(T.IK[:, :], 128, [[-16, 8], [0, 16]], 0, 1, ("IK", 0, 128))
-    pool(T.II[:, :], 128, [[-1, 128]], 0, 1, ("II", 0, 128))
+    pool(T.II[:, :], 144, [[-1, 144]], 0, 1, ("II", 0, 144))
     pool(T.IP[:, 0:1], 1, [[0, 1]], 0, 1, ("IP", 0, 1))
+    pool(T.IK[:, :], 128, [[-16, 8], [0, 16]], 0, 1, ("IK", 0, 128))
     pool(T.IM[:, :], 64, [[16, 64]], 0, 0, ("IM", 0, 64))
-    send_values(0, ("W0", 0, GH))
-    pool(T.IZ[:, :], 144, [[-1, 16], [-16, 9]], 0, 1, ("IZ", 0, 144))
-    pool(T.X0[:, :], P, [[1, P]], OWN[0], 0, ("X0", 0, P), True)
+    send_values(0, ("W0", B0, B0 + GH))
+    pool(T.IZ[:, :], 72, [[-2, 8], [-16, 9]], 0, 1, ("IZ", 0, 72))
+    pool(T.X0[:, :], P, [[1, P]], OWN[0] - B0 - OFF[1], 0, ("X0", 0, P), True)
 
-    cp(("SU", 0, P), ("SI", 0, P))
-    cp(("SW0", 0, P), ("SI", 0, P))
+    ts(("IP", 2, 3), ("IP", 0, 1), 15, None, ALU.bitwise_and)
+    ts(("IP", 4, 5), ("IP", 0, 1), 1, None, ALU.bitwise_and)
+    cp(col(1), ("IP", 4, 5))
+    cp(col(0), ("IP", 2, 3))
+    ts(col(2), col(1), -1.0, 1.0, ALU.mult, ALU.add)
+    ts(col(3), col(1), float(OFF[0] - OFF[1]), float(-OFF[0]), ALU.mult, ALU.add)
+    for e in range(2):
+        ts(("R%d" % e, 0, 144), ("II", 0, 144), float(e - 1), col(2 - e), ALU.is_equal, ALU.mult)
+    for n0, n1 in ((0, GH), (GH, P)):
+        ts(("S16", n0, n1), ("SI", n0, n1), col(3), None, ALU.add)
+        for e in range(2):
+            bank = "P%d" % (4 + e)
+            mm(fold(e, "S16", n0, n1, n0 // 2, True), [("R%d" % e, 0, 144), ("S16", n0, n1)], bank)
+            cp(("H%d" % e, n0 // 2, n1 // 2), (bank, n0 // 2, n1 // 2))
+            ts(("HU%d" % e, n0 // 2, n1 // 2), ("H%d" % e, n0 // 2, n1 // 2), float(OFF[e]), None, ALU.add)
+    ts(("TM", 0, 256), ("SI", 0, 256), float(GH), -BIG, ALU.is_ge, ALU.mult)
+    tt(("TS0", 0, 256), ("TM", 0, 256), ("SI", 0, 256), ALU.add)
+    send_tuples(0)
     ts(("IK2", 0, 128), ("IK", 0, 128), 4, None, ALU.arith_shift_right)
     ts(("E", 0, 128), ("IK2", 0, 128), 0.0, None, ALU.is_equal)
     ts(("ID", 0, 128), ("II", 0, 128), 0.0, None, ALU.is_equal)
+    cp(("I16", 0, 128), ("ID", 0, 128))
     op("v", 64 + OVH, lambda e: V.tensor_scalar(T.GM[:, :], T.E[:, 0:128:16], 1.0 / 256, None, ALU.mult),
        [("E", 0, 128)], [("GM", 0, 8)])
     for a in range(8):
-        if a < 4:
-            fn = lambda e, a=a: V.tensor_scalar(T.MB[:, :, a, :], T.MT[:, :], T.GM[:, a:a + 1], None, ALU.mult)
-        else:
-            fn = lambda e, a=a: S.activation(T.MB[:, :, a, :], T.MT[:, :], ACT.Identity, scale=T.GM[:, a:a + 1])
-        op("v" if a < 4 else "a", (128 if a < 4 else 256) + OVH, fn, [("MT", 0, 256), ("GM", 0, 8)], [("MB", a, a + 1)])
-    ts(("IP", 2, 3), ("IP", 0, 1), 15, None, ALU.bitwise_and)
-    ts(("IP", 4, 5), ("IP", 0, 1), 1, None, ALU.bitwise_and)
-    cp(("COL", 0, 1), ("IP", 2, 3))
-    cp(("COL", 1, 2), ("IP", 4, 5))
-    ts(("COL", 2, 3), ("COL", 1, 2), 257.0, -1.0, ALU.mult, ALU.add)
-    ts(("COL", 3, 4), ("COL", 1, 2), -1536.0, 1535.5, ALU.mult, ALU.add)
-    ts(("COL", 4, 5), ("COL", 1, 2), 1792.0, -0.5, ALU.mult, ALU.add)
-    ts(("COL", 5, 6), ("COL", 0, 1), 0.0, 64.0, ALU.is_equal, ALU.mult)
-    ts(("COL", 6, 7), ("COL", 0, 1), 1.0, None, ALU.is_equal)
-    tt(("COL", 7, 8), ("COL", 5, 6), ("COL", 6, 7), ALU.add)
-    ts(("IL", 0, 64), ("IM", 0, 64), ("COL", 0, 1), None, ALU.add)
+        fn = lambda e, a=a: S.activation(T.MB[:, :, a, :], T.MT[:, :], ACT.Identity, scale=T.GM[:, a:a + 1])
+        op("a", 256 + OVH, fn, [("MT", 0, 256), ("GM", 0, 8)], [("MB", a, a + 1)])
+    ts(("IL", 0, 64), ("IM", 0, 64), col(0), None, ALU.add)
     fill(("ZB", 0, 144), 0.0)
     op("v", 64 + OVH, lambda e: V.tensor_copy(T.ZB[:, 15:143:16], T.E[:, 0:128:16]), [("E", 0, 128)], [("ZB", 0, 144)])
+    fill(("ZR", 0, 1152), 0.0)
+    for h in range(2):
+        op("v", 72 + OVH, lambda e, h=h: V.tensor_scalar(T.ZR[:, 14 + h:1152:16], T.IZ[:, :], float(h), None, ALU.is_equal),
+           [("IZ", 0, 72)], [("ZR", 0, 1152)])
     ts(("ZK", 0, 144), ("ZB", 0, 144), 65536.0, None, ALU.mult)
-    ts(("ZH", 0, 144), ("ZB", 0, 144), ("COL", 7, 8), None, ALU.mult)
-    fill(("ZR", 0, 2304), 0.0)
-    op("v", 144 + OVH, lambda e: V.tensor_scalar(T.ZR[:, 15:2304:16], T.IZ[:, :], 0.0, None, ALU.is_equal),
-       [("IZ", 0, 144)], [("ZR", 0, 2304)])
-    cp(("Z32", 0, 144), ("ZR", 5 * 144, 6 * 144))
-    cp(("Z32", 144, 288), ("ZR", 11 * 144, 12 * 144))
-    ts(("PEN", 0, 128), ("E", 0, 128), -4096.0, None, ALU.mult)
+    ts(("IO", 0, 4), ("II", 0, 4), 15, None, ALU.bitwise_and)
+    ts(("OH", 0, 4), ("IO", 0, 4), 0.0, None, ALU.is_equal)
+    ts(col(4), ("OH", 0, 1), 64.0, ("OH", 1, 2), ALU.mult, ALU.add)
+    for k, (z, row, wt) in enumerate((("ZA", 3, -2304.0), ("ZC", 3, 1024.0), ("ZP", 2, BIG), ("ZM", 2, -BIG))):
+        ts(col(5 + k), ("OH", row, row + 1), wt, col(4), ALU.mult, ALU.add)
+        scale((z, 0, 144), ("ZB", 0, 144), col(5 + k))
+    scale(("ZH", 0, 144), ("ZB", 0, 144), col(4))
+    scale(("EN", 0, 128), ("E", 0, 128), col(4))
+    for z, wt in (("EM", -BIG), ("EP", BIG)):
+        fill((z, 0, 144), 0.0)
+        op("v", 64 + OVH, lambda e, z=z, wt=wt: V.tensor_scalar(T[z][:, 1:129:2], T.E[:, 0:128:2], wt, None, ALU.mult),
+           [("E", 0, 128)], [(z, 0, 144)])
+    ts(("PEN", 0, 128), ("E", 0, 128), -BIG, None, ALU.mult)
     ts(("NL", 0, 128), ("ID", 0, 128), 4096.0, None, ALU.mult)
     tt(("LM", 0, 128), ("NL", 0, 128), ("E", 0, 128), ALU.max)
     ts(("NL", 0, 128), ("LM", 0, 128), -1.0, None, ALU.mult)
     fill(("CH", 0, 512), -1152.0)
-    cp(("I16", 0, 128), ("ID", 0, 128))
     fill(("CN", 0, 32), 0.0)
     fill(("CN", 32, 96), -983040.0)
-    fill(("CB1", 0, 256), float(P + GH))
-    fill(("CB2", 0, 256), float(P + 2 * GH))
-    ts(("S16", 0, P), ("SU", 0, P), float(-OFF16), None, ALU.add)
-    ts(("TM", 0, 256), ("SI", 0, 256), ("COL", 2, 3), None, ALU.is_lt)
-    ts(("TV", 0, 256), ("SI", 0, 256), float(P), None, ALU.add)
-    tt(("TS0", 0, 256), ("TM", 0, 256), ("TV", 0, 256), ALU.mult)
-    send_tuples(0)
-    pool(T.HL[0:64, :], 2304, [[1, 36], [0, 64]], 0, 0, ("HL", 0, 2304, 0), True)
-    pool(T.HL[64:128, :], 2304, [[0, 36], [1, 64]], 0, 0, ("HL", 0, 2304, 1), True)
-    pool(T.X1[:, :], P, [[1, P]], OWN[1], 0, ("X1", 0, P), True)
-    pool(T.X2[:, :], P, [[1, P]], OWN[2], 0, ("X2", 0, P), True)
-    for h in range(2):
-        dma(T.FT[h:128:2, 0:2304], T.HL[64 * h:64 * h + 64, :], [("HL", 0, 2304, h)], [("FT", 0, 2304, h)])
-    dma(T.DTa[:, P:2304], T.FT[:, P:2304], [("FT", P, 2304)], [("DTa", P, 2304)])
-    dma(T.DTb[:, P:2304], T.FT[:, P:2304], [("FT", P, 2304)], [("DTb", P, 2304)])
-    dma(T.FT[:, 2304:3328], T.FT[:, 0:P], [("FT", 0, P)], [("FT", 2304, 3328)])
-    dma(T.FT[:, 3328:5632], T.FT[:, 0:2304], [("FT", 0, 2304)], [("FT", 3328, 5632)])
+    pool(T.HL[0:32, :], 2304, [[1, 36], [0, 64]], 0, 0, ("HL", 0, 2304, 0), True)
+    pool(T.HL[32:64, :], 2304, [[0, 36], [1, 64]], 0, 0, ("HL", 0, 2304, 1), True)
+    for r, cut in ((2, GH), (3, P)):
+        pool(T.HL[32 * r:32 * r + 32, 0:cut], cut, [[0, cut]], 0, 0, ("HL", 0, cut, r), True)
+        pool(T.HL[32 * r:32 * r + 32, cut:2304], 2304 - cut, [[0, 2304 - cut]], 1, 0, ("HL", cut, 2304, r), True)
+    pool(T.X1[:, :], P, [[1, P]], OWN[1] - B0 - OFF[0], 0, ("X1", 0, P), True)
+    pool(T.X2[:, :], P, [[1, P]], OWN[2] - B0 - OFF[1], 0, ("X2", 0, P), True)
+    pool(T.F[:, GO:B1], B1 - GO, [[1, B1 - GO]], P, 0, ("F", GO, B1), True)
+    for r in range(4):
+        dma(T.FT[r:128:4, B0:B1], T.HL[32 * r:32 * r + 32, :], [("HL", 0, 2304, r)], [("FT", B0, B1, r)])
+    copy(("DTa", P, 2304), ("FT", GO, B1))
+    copy(("DTb", P, 2304), ("FT", GO, B1))
+    copy(("FT", B1, END), ("FT", B0, GO))
+    copy(("FT", B2, B0), ("FT", B0, GO))
+    copy(("W2", B0, GO), ("W0", B0, GO))
 
     def guests(src):
-        tolist("P7", 0, "ZB", 0, src)
+        tolist("P7", 0, "ZB", src)
         tt(("GI", 0, 64), ("P7", 0, 64), ("IL", 0, 64), ALU.add)
         ts(("GJ", 0, 64), ("GI", 0, 64), GH - 1, None, ALU.bitwise_and)
         cp(("GL", 0, 64), ("GJ", 0, 64))
 
-    def klist(t, ks, sw):
-        wide = t == 2 and ks[0] == 1
-        for k in ks:
-            if wide:
-                tolist("P4", 64 * k, "Z32", 144 * (k // 2), (sw, 0, P), slow=4)
-            else:
-                tolist("P4", 64 * k, "ZR", 144 * (3 * k + t), ("S16", 0, P))
-            off = 0.0 if wide else float(OFF16)
-            ts(("KL", 64 * k, 64 * k + 64), ("P4", 64 * k, 64 * k + 64), off, None, ALU.add)
-            act(("KY", 64 * k, 64 * k + 64), ("P4", 64 * k, 64 * k + 64), ACT.Identity, off + 8192.0 * (5 - k))
+    def lists(t, rows, bank, dst):
+        off = float(OFF[rows[0] % 2] + B0 - BASE[t])
+        for j, o in enumerate(rows):
+            rowlist(bank, 64 * j, o)
+        ts((dst[0], dst[1], dst[1] + 64 * len(rows)), (bank, 0, 64 * len(rows)), off, None, ALU.add)
+        for j, o in enumerate(rows):
+            if o % 3 == t and o // 3 < 5:
+                k = o // 3
+                act(("KY", 64 * k, 64 * k + 64), (bank, 64 * j, 64 * j + 64), ACT.Identity, off + 8192.0 * (5 - k))
+
+    FIN = [2, 8, 14, 0, 4, 6, 10, 12, 5, 11, 1, 3, 7, 9, 13, 15]
+
+    def klist(t, k):
+        if t + 1 < RO:
+            c = 64 * [0, 3, 1, 4, 2][k]
+            return "KL", c
+        return "FL", 64 * FIN.index(3 * k + t)
+
+    def early(t):
+        lists(t, [t, t + 6, t + 12], "P4", ("KL", 0) if t + 1 < RO else ("FL", 0))
 
     def compose(buf, t):
         if t == 2:
-            gat2((buf, 2304, 3328), (buf, 3328, 5632), ("LB", 0, 64))
+            gat2((buf, B1, END), (buf, B2, B1), ("LB", 0, 64))
         if t >= 1:
-            gat2((buf, 0, P), (buf, P, 3328), ("LA", 0, 64))
+            gat2((buf, B0, GO), (buf, GO, END), ("LA", 0, 64))
 
     def one_round(t):
-        W, sw, sn, X, TG = "W%d" % t, "SW%d" % (t % 2), "SW%d" % ((t + 1) % 2), "X%d" % t, "TG%d" % t
+        W, X, TG = "W%d" % t, "X%d" % t, "TG%d" % t
         par = (t + 1) % 2
         own = OWN[t]
+        H, HU = "H%d" % par, "HU%d" % par
+        copy(("UW", GO, B1), (W, GO, B1))
         vb, v0 = ("W%d" % (t + 1), OWN[t + 1]) if t + 1 < RO else ("VN", 0)
-        dma(T[X][1 - par:128:2, :], T[sw][1 - par:128:2, 0:P], [(sw, 0, P)], [(X, 0, P)])
-        dma(T.UW[:, P:2304], T[W][:, P:2304], [(W, P, 2304)], [("UW", P, 2304)])
-        if t == 2:
-            dma(T.UW[:, 4352:5632], T[W][:, P:2304], [(W, P, 2304)], [("UW", 4352, 5632)])
 
-        def cands(b):
-            gtt((sw, P + 512 * b, P + 512 * b + 512), (TG, 0, 256), ("GL", 32 * b, 32 * b + 32), (X, 512 * b, 512 * b + 512),
-                ALU.max if t == 0 else ALU.min)
-            for h in range(2):
-                pp = par if h == 0 else 1 - par
-                lo = P + 512 * b + 256 * h
-                dma(T.C2f[pp:128:2, 256 * b:256 * b + 256], T[sw][par:128:2, lo:lo + 256], [(sw, lo, lo + 256)],
-                    [("C2f", 256 * b, 256 * b + 256, pp)])
-            cp(("C2u", 256 * b, 256 * b + 256), ("C2f", 256 * b, 256 * b + 256))
+        def arcs(buf, lst, win, e, n0, n1, banks, ch):
+            ch = min(ch, (n1 - n0) // 2)
+            for c0 in range(n0 // 2, n1 // 2, ch):
+                x = (buf, 16 * c0, 16 * (c0 + ch))
+                gat(x, win, (lst, c0, c0 + ch))
+                lo = 2 * c0 - n0
+                for bank in banks:
+                    mm([(lo + s % 2, lo + 2 * ch, T.MB[:, s - s % 2 + e, :, :], T[buf][:, x[1] + s:x[2]:16], False)
+                        for s in range(16)], [x, ("MB", 0, 16)], bank, step=2)
 
-        def old(c0, half, bank, stop=False):
-            mm([(c0 % 512, c0 % 512 + ACH, T.MB[:, o, :, :], T.GA[:, 16 * c0 + o:16 * (c0 + ACH):16], False)
-                for o in range(half, 16, 2)], [("GA", 16 * c0, 16 * (c0 + ACH)), ("MB", 0, 8)], bank, stop=stop)
+        def kept(j):
+            n0, n1 = CHUNKS[j]
+            for bank in BANKS[j]:
+                mm([(0, n1 - n0, T.ID[:, :], T.RW[:, n0:n1], True)], [("ID", 0, 128), ("RW", n0, n1)], bank)
+            arcs("GX", "HU%d" % (1 - par), (W, B0, STOP[t]), 1 - par, n0, n1, BANKS[j], XCH)
+            arcs("GY", HU, (W, B0, STOP[t]), par, n0, n1, BANKS[j][:1], GCH)
+            ts(("AI", n0, n1), (BANKS[j][0], 0, n1 - n0), 255.25, -255.0 / 512, ALU.min, ALU.add)
 
-        def kept(b, lo, hi):
-            for c0 in range(512 * b + lo, 512 * b + hi, ACH):
-                gat(("GA", 16 * c0, 16 * (c0 + ACH)), (W, 0, WIN[t]), ("SU", c0, c0 + ACH))
-                old(c0, 1 - par, "A%d" % b)
-                old(c0, par, "A%d" % b, c0 % 512 + ACH == 512)
-                old(c0, 1 - par, "B%d" % b)
+        def cands(j):
+            n0, n1 = CANDS[j]
+            gtt(("CG", n0, n1), (TG, 0, 256), ("GL", n0 // 16, n1 // 16), (X, n0, n1), ALU.min if t == 1 else ALU.max)
+            mm(fold(par, "CG", n0, n1, n0 // 2, True), [("R%d" % par, 0, 144), ("CG", n0, n1)], "P5")
+            ts(("CU", n0 // 2, n1 // 2), ("P5", n0 // 2, n1 // 2), float(OFF[par] + B0 - BASE[t]), None, ALU.add)
 
-        def worth(b):
-            ts(("AI", 512 * b, 512 * b + 512), ("A%d" % b, 0, 512), 255.25, -255.0 / 512, ALU.min, ALU.add)
-
-        def choose(b):
-            bank = "B%d" % b
-            for c0 in range(256 * b, 256 * b + 256, BCH):
-                gat(("GB", 16 * c0, 16 * (c0 + BCH)), (W, 0, WIN[t]), ("C2u", c0, c0 + BCH))
-                m0 = c0 % 256
-                it = []
-                for s in range(16):
-                    h = 0 if s % 2 == par else 1
-                    o = s if h == 0 else s ^ 1
-                    it.append((256 * h + m0, 256 * h + m0 + BCH, T.MB[:, o, :, :], T.GB[:, 16 * c0 + s:16 * (c0 + BCH):16],
-                               False))
-                mm(it, [("GB", 16 * c0, 16 * (c0 + BCH)), ("MB", 0, 8)], bank, stop=m0 + BCH == 256)
-            lo, hi = 512 * b, 512 * b + 512
-            tt(("LT", lo, hi), (bank, 0, 512), ("AI", lo, hi), ALU.is_lt)
-            ts(("B16", lo, hi), (bank, 0, 512), 255.25, 1152 - 255.0 / 512, ALU.min, ALU.add)
-            bank = "A%d" % b
-            mm([(0, 512, T.ID[:, :], T.CH[:, :], True), (0, 512, T.PEN[:, :], T.LT[:, lo:hi], False)],
-               [("PEN", 0, 128), ("LT", lo, hi), ("ID", 0, 128), ("CH", 0, 512)], bank, stop=False)
-            mm([(0, 512, T.I16[:, :], T.B16[:, lo:hi], False)], [("I16", 0, 128), ("B16", lo, hi)], bank)
-            tt(("UW", own + lo, own + hi), (bank, 0, 512), ("AI", lo, hi), ALU.max)
-            if b == 0:
-                dma(T[vb][:, v0:v0 + 512], T.UW[:, own:own + 512], [("UW", own, own + 512)], [(vb, v0, v0 + 512)])
-            else:
-                cp((vb, v0 + lo, v0 + hi), ("UW", own + lo, own + hi))
-            if b == 0 and t + 1 < RO:
-                send_values(t + 1, ("UW", own, own + GH))
-            x, y = 32 * b, 32 * b + 32
-            tolist("P6", x, "ZB", 0, ("LT", lo, hi))
-            ts(("OA", x, y), ("P6", x, y), 0.0, float(P), ALU.is_equal, ALU.mult)
-            tt(("OB", x, y), ("OA", x, y), ("IL", x, y), ALU.add)
-            cp(("OL", x, y), ("OB", x, y))
-            gat((sn, lo, hi), (sw, 0, 2 * P), ("OL", x, y))
-            cp(("SU", lo, hi), (sn, lo, hi))
+        def choose(j):
+            n0, n1 = CHUNKS[j]
+            w, x, y = n1 - n0, n0 // 2, n1 // 2
+            a, b = BANKS[j]
+            arcs("GZ", "CU", (W, BASE[t], B1 if t == 2 else STOP[t]), par, n0, n1, [b], GCH)
+            mm([(0, w, T.ID[:, :], T.CH[:, 0:w], True)], [("ID", 0, 128), ("CH", 0, 512)], a)
+            tt(("LT", n0, n1), (b, 0, w), ("AI", n0, n1), ALU.is_lt)
+            ts(("B16", n0, n1), (b, 0, w), 255.25, 1152 - 255.0 / 512, ALU.min, ALU.add)
+            mm([(0, w, T.PEN[:, :], T.LT[:, n0:n1], False)], [("PEN", 0, 128), ("LT", n0, n1)], a)
+            mm([(0, w, T.I16[:, :], T.B16[:, n0:n1], False)], [("I16", 0, 128), ("B16", n0, n1)], a)
+            tt(("UW", own + n0, own + n1), (a, 0, w), ("AI", n0, n1), ALU.max)
             if t + 1 < RO:
-                ts(("S16", lo, hi), ("SU", lo, hi), float(-OFF16), None, ALU.add)
-            if t + 1 < RO and b == 0:
-                for h in range(2):
-                    pp = (1 - par) if h == 0 else par
-                    dma(T.SNf[pp:128:2, :], T[sn][1 - par:128:2, 128 * h:128 * h + 128], [(sn, 128 * h, 128 * h + 128)],
-                        [("SNf", 0, 128, pp)])
-                cp(("SNu", 0, 128), ("SNf", 0, 128))
+                if n0 == 0:
+                    send_values(t + 1, ("UW", own, own + GH))
+            (copy if n1 < P else cp)((vb, v0 + n0, v0 + n1), ("UW", own + n0, own + n1))
+            if t + 1 == RO:
+                dma(T.yv[:, n0:n1], T.UW[:, own + n0:own + n1], [("UW", own + n0, own + n1)], [])
+            for lo, z in ((0, "EM"), (256, "EP")):
+                it = fold(par, "CG", n0, n1, lo, True)
+                it += [(lo, lo + w // 2, T[z][:, 1 - h:129 - h], T.LT[:, n0 + h:n1:2], False) for h in range(2)]
+                mm(it, [("R%d" % par, 0, 144), ("CG", n0, n1), (z, 0, 144), ("LT", n0, n1)], b)
+            tt(("TT", x, y), (b, 0, w // 2), (H, x, y), ALU.max)
+            tt((H, x, y), (b, 256, 256 + w // 2), ("TT", x, y), ALU.min)
+            if t + 1 < RO:
+                ts((HU, x, y), (H, x, y), float(OFF[par]), None, ALU.add)
 
-        for b in range(2):
-            for bank in ("A%d" % b, "B%d" % b):
-                mm([(0, 512, T.ID[:, :], T.RW[:, 512 * b:512 * b + 512], True)],
-                   [("ID", 0, 128), ("RW", 512 * b, 512 * b + 512)], bank, stop=False)
-        kept(0, 0, 512)
-        worth(0)
-        cands(0)
-        cands(1)
-        kept(1, 0, 256)
-        choose(0)
-        kept(1, 256, 512)
-        worth(1)
-        choose(1)
+        for j in range(len(CANDS)):
+            cands(j)
+        for j in range(len(CHUNKS)):
+            kept(j)
+        for j in range(len(CHUNKS)):
+            choose(j)
         vn = ("UW", own, own + P)
-        if t == 1:
-            dma(T.W2[:, 4352:5632], T.W2[:, P:2304], [("W2", P, 2304)], [("W2", 4352, 5632)])
-        if t + 1 == RO:
-            dma(T.yv[:, :], ap(vn), [vn], [])
         compose("UW", t)
-        klist(t, [1, 3], sn)
-        act(("AC", 0, 64), ("IL", 0, 64), ACT.Identity, float(own))
-        uw = ("UW", 0, WIN[t])
+        lists(t, [t + 3, t + 9], "P5", ("KL", 192) if t + 1 < RO else ("FL", 512))
+        acc = ("IL", 0, 64)
+        if own != BASE[t]:
+            acc = ("AC", 0, 64)
+            act(acc, ("IL", 0, 64), ACT.Identity, float(own - BASE[t]))
+        uw = ("UW", BASE[t], STOP[t])
         for j, k in enumerate(KORD):
-            df, bank, col, way = "DF%d" % k, ("P5" if j % 2 == 0 else "P6"), 64 * (k + 1), WAYS[k]
+            df, bank, c, way = "DF%d" % k, ("P7" if j % 2 == 0 else "P6"), 64 * (k + 1), WAYS[k]
+            kb, kc = klist(t, k)
             for b in range(2):
                 lo, hi, bk = 512 * b, 512 * b + 512, ("A%d" if k == 0 else "B%d") % b
-                kl = ("KL", 64 * k + 32 * b, 64 * k + 32 * b + 32)
+                kl = (kb, kc + 32 * b, kc + 32 * b + 32)
                 if way[b] == "a":
                     sg = "SG%d" % (j % 2)
                     gat((sg, lo, hi), uw, kl, eng="a")
@@ -371,65 +400,70 @@ def build(g, core, T, topo):
                        [("NL", 0, 128), ("LM", 0, 128), ("UW", own + lo, own + hi), (sg, lo, hi)], bk)
                     act((df, lo, hi), (bk, 0, 512), ACT.Sign, -0.5)
                 elif way == "vv" and b == 0:
-                    gtt((df, 0, P), uw, ("KL", 64 * k, 64 * k + 64), (vb, v0, v0 + P), ALU.subtract)
+                    gtt((df, 0, P), uw, (kb, kc, kc + 64), (vb, v0, v0 + P), ALU.subtract)
                     ts((df, 0, P), (df, 0, P), 16.0, 1.0, ALU.mult, ALU.min)
                 elif way != "vv":
                     gtt((df, lo, hi), uw, kl, (vb, v0 + lo, v0 + hi), ALU.subtract)
                     ts((df, lo, hi), (df, lo, hi), 16.0, 1.0, ALU.mult, ALU.min)
-            tolist(bank, col, "ZK", 0, (df, 0, P), tail={"aa": ("CN", 32, 96), "va": ("CN", 0, 64), "vv": None}[way])
-            tt(("ZZ", 64 * k, 64 * k + 64), (bank, col, col + 64), ("KY", 64 * k, 64 * k + 64), ALU.min)
+            tolist(bank, c, "ZK", (df, 0, P), tail={"aa": ("CN", 32, 96), "va": ("CN", 0, 64), "vv": None}[way])
+            tt(("ZZ", 64 * k, 64 * k + 64), (bank, c, c + 64), ("KY", 64 * k, 64 * k + 64), ALU.min)
             nxt = ("AJ", 0, 64) if j == 4 else ("AC", 64 * j + 64, 64 * j + 128)
-            tt(nxt, ("AC", 64 * j, 64 * j + 64), ("ZZ", 64 * k, 64 * k + 64), ALU.max)
+            tt(nxt, acc, ("ZZ", 64 * k, 64 * k + 64), ALU.max)
+            acc = nxt
         ts(("AK", 0, 64), ("AJ", 0, 64), 8191, None, ALU.bitwise_and)
         cp(("DR", 0, 64), ("AK", 0, 64))
-        gat2(("DTa", 0, P), ("FT", 0, WIN[t]), ("DR", 0, 64))
+        gat2(("DTa", 0, P), ("FT", BASE[t], STOP[t]), ("DR", 0, 64))
         d1 = ("DR", 0, 64)
         if t > 0:
-            tolist("P6", 448, "ZH", 0, ("DTa", 0, P))
+            tolist("P6", 448, "ZH", ("DTa", 0, P))
             d1 = ("D1", 0, 64)
             cp(d1, ("P6", 448, 512))
         if t + 1 < RO:
             guests(vn)
-            klist(t + 1, [0, 2, 4], None)
+            early(t + 1)
+        else:
+            lists(t, FIN[3:8], "P4", ("FL", 192))
+            lists(t, FIN[10:16], "P5", ("FL", 640))
         gat2(("DTb", 0, P), ("DTa", 0, 2304), d1)
-        gat2(("DTa", 0, P), ("DTb", 0, 2304), d1)
-        gat2(("FT", own, own + P), ("DTa", 0, 2304), d1)
+        tolist("P6", 448, "ZH", ("DTb", 0, P))
+        cp(("D2", 0, 64), ("P6", 448, 512))
         if t + 1 < RO:
-            tolist("P5", 448, "ZH", 0, ("FT", own, own + P))
+            gat2(("FT", own, own + P), ("DTb", 0, 2304), ("D2", 0, 64))
             if t == 0:
-                ts(("LC", 0, 64), ("P5", 448, 512), float(P), 2304.0, ALU.is_lt, ALU.mult)
-                tt(("LD", 0, 64), ("P5", 448, 512), ("LC", 0, 64), ALU.add)
-                ts(("LA", 0, 64), ("LD", 0, 64), float(-P), None, ALU.add)
+                tolist("P7", 448, "ZA", ("FT", own, own + P))
+                ts(("LA", 0, 64), ("P7", 448, 512), 1280.0, None, ALU.add)
             else:
-                cp(("LB", 0, 64), ("P5", 448, 512))
-                gat2(("FT", 0, P), ("FT", P, 3328), ("LA", 0, 64))
-            for h in range(2):
-                gat(("GS", P * h, P * h + P), ("FT", 0, WIN[t]), ("SNu", 64 * h, 64 * h + 64))
-            cb = "CB%d" % (t + 1)
-            it = [(64, 320, T.ID[:, :], T[cb][:, :], True)]
-            for s in range(16):
-                h = 0 if s % 2 == 1 - par else 1
-                o = s if h == 0 else s ^ 1
-                it.append((64 + 128 * h, 192 + 128 * h, T.ZH[:, 15 - o:143 - o], T.GS[:, s:2048:16], False))
-            mm(it, [("ID", 0, 128), (cb, 0, 256), ("ZH", 0, 144), ("GS", 0, 2048)], "P7")
-            ts(("TM", 0, 256), ("P7", 64, 320), ("COL", 3 + t, 4 + t), 8192.0, ALU.is_ge, ALU.mult)
-            tt(("TS%d" % (t + 1), 0, 256), ("P7", 64, 320), ("TM", 0, 256), ALU.add)
-            send_tuples(t + 1)
+                tolist("P7", 448, "ZC", ("FT", own, own + P))
+                cp(("LB", 0, 64), ("P7", 448, 512))
+                gat2(("FT", B0, GO), ("FT", GO, END), ("LA", 0, 64))
             compose("W%d" % (t + 1), t + 1)
+            for h in range(2):
+                gat(("GS", P * h, P * h + P), ("FT", B0, B1), ("HU%d" % (1 - par), 64 * h, 64 * h + 64))
+            z = "ZP" if t == 0 else "ZM"
+            it = []
+            for s in range(16):
+                o = s - s % 2 + 1 - par
+                it.append((64 + s % 2, 320, T[z][:, 15 - o:143 - o], T.GS[:, s:2048:16], s == 0))
+            mm(it, [(z, 0, 144), ("GS", 0, 2048)], "P7", step=2)
+            move(("TS%d" % (t + 1), 0, 256), ("P7", 64, 320), float(P + GH * (t + 1) - OFF[1 - par]))
+            send_tuples(t + 1)
+        else:
+            for b in range(2):
+                mm([(0, 512, T.EN[:, :], T.DTb[:, 512 * b:512 * b + 512], True)], [("EN", 0, 128), ("DTb", 512 * b, 512 * b + 512)],
+                   "A%d" % b)
+                move(("F", B0 + 512 * b, B0 + 512 * b + 512), ("A%d" % b, 0, 512))
+            gat2(("F", B2, B0), ("F", B0, B1), ("D2", 0, 64))
+            compose("F", t)
 
-    guests(("W0", 0, P))
-    klist(0, [0, 2, 4], None)
+    guests(("W0", B0, GO))
+    early(0)
     for t in range(RO):
         one_round(t)
-    compose("FT", 2)
-    for j, (c0, w) in enumerate(LAST):
-        bank = PSUM[j % 4]
-        gat(("GA", 16 * c0, 16 * (c0 + w)), ("FT", 0, WIN[2]), ("SU", c0, c0 + w))
-        mm([(0, w, T.ZH[:, 15 - o:143 - o], T.GA[:, 16 * c0 + o:16 * (c0 + w):16], o == 0) for o in range(16)],
-           [("ZH", 0, 144), ("GA", 16 * c0, 16 * (c0 + w))], bank)
-        move(("YS", c0, c0 + w), (bank, 0, w))
-        if j % 2 == 1:
-            dma(T.ys[:, c0 - w:c0 + w], T.YS[:, c0 - w:c0 + w], [("YS", c0 - w, c0 + w)], [])
+    for j, o in enumerate(FIN):
+        s = P * (j % SLOTS)
+        for lo, hi in ((0, P),) if j < 14 else ((0, 512), (512, P)):
+            gat(("FO", s + lo, s + hi), ("F", B2, END), ("FL", 64 * j + lo // 16, 64 * j + hi // 16))
+            dma(T.ys[o:128:16, lo:hi], T.FO[0:128:16, s + lo:s + hi], [("FO", s + lo, s + hi)], [])
     return ops
 
 
@@ -456,6 +490,7 @@ def order(ops):
 
     def place(key, pick):
         key = list(key)
+        pick = list(pick)
         for i in range(n):
             for j in pre[i]:
                 if key[j] >= key[i]:
@@ -463,24 +498,32 @@ def order(ops):
         busy = {e: [] for e in "vapgsx"}
         start, end, why = [0.0] * n, [0.0] * n, [-1] * n
         for i in sorted(range(n), key=lambda i: key[i]):
-            s, w = 0.0, -1
+            s0, w0 = 0.0, -1
             for j, d in near[i]:
-                if end[j] + d > s:
-                    s, w = end[j] + d, j
-            q = busy[pick[i]]
-            k = len(q)
-            while k and q[k - 1][1] > s:
-                k -= 1
-            while k < len(q) and s + hold[i] > q[k][0]:
-                if q[k][1] > s:
-                    s, w = q[k][1], q[k][2]
-                k += 1
-            q.insert(k, (s, s + hold[i], i))
+                if end[j] + d > s0:
+                    s0, w0 = end[j] + d, j
+            got = None
+            for e in pick[i]:
+                s, w, q = s0, w0, busy[e]
+                k = len(q)
+                while k and q[k - 1][1] > s:
+                    k -= 1
+                while k < len(q) and s + hold[i] > q[k][0]:
+                    if q[k][1] > s:
+                        s, w = q[k][1], q[k][2]
+                    k += 1
+                if got is None or s <= got[0]:
+                    got = (s, w, k, e)
+            s, w, k, pick[i] = got
+            busy[pick[i]].insert(k, (s, s + hold[i], i))
             start[i], end[i], why[i] = s, s + cost[i], w
-        return start, end, why
+        return (start, end, why), pick
 
-    pick = [o["eng"][-1] if i % 5 < 3 else o["eng"][0] for i, o in enumerate(ops)]
-    res = place(range(n), pick)
+    rest = list(cost)
+    for i in range(n - 1, -1, -1):
+        for j, d in near[i]:
+            rest[j] = max(rest[j], cost[j] + d + rest[i])
+    res, pick = place([-x for x in rest], [o["eng"] for o in ops])
     best = (res, pick)
     x = SEED
     for it in range(TRIES):
@@ -511,12 +554,114 @@ def order(ops):
                     if key[b] >= key[a]:
                         key[b] = key[a] - 1e-3
                         stack.append(b)
-        r2 = place(key, p2)
+        r2, p2 = place(key, p2)
         if max(r2[1]) <= max(res[1]) + SLACK * (1 - it / TRIES):
             res, pick = r2, p2
             if max(res[1]) < max(best[0][1]):
                 best = (res, pick)
     return pre, best[0][0], best[0][1], best[1]
+
+
+def order(ops):
+    n = len(ops)
+    pre = [set() for _ in range(n)]
+    seen = {}
+    for i, o in enumerate(ops):
+        if o["after"] is not None:
+            pre[i].add(o["after"])
+        for x, wr in [(x, False) for x in o["r"]] + [(x, True) for x in o["w"]]:
+            lst = seen.setdefault(x[0], [])
+            if x[0] in PSUM:
+                for j, y, wy in reversed(lst):
+                    add = ops[j]["cls"] == "add"
+                    if not (add and o["cls"] == "add"):
+                        pre[i].add(j)
+                    if not add:
+                        break
+                continue
+            for j, y, wy in lst:
+                if (wr or wy) and _conf(x, y):
+                    pre[i].add(j)
+        for x in o["r"]:
+            seen[x[0]].append((i, x, False))
+        for x in o["w"]:
+            seen[x[0]].append((i, x, True))
+    pre = [sorted(x) for x in pre]
+    cost = [o["cost"] for o in ops]
+    hold = [{"c": o["cost"], "d": 100.0, "r": 600.0, "x": 0.0}[o["kind"]] for o in ops]
+    engs = [o["eng"] for o in ops]
+    fw = [[] for _ in range(n)]
+    bw = [[] for _ in range(n)]
+    for i in range(n):
+        for j in pre[i]:
+            d = 0.0 if engs[i] == "p" and engs[j] == "p" else LAT
+            fw[i].append((j, d + cost[j]))
+            bw[j].append((i, d + hold[i] + cost[j] - hold[j]))
+
+    def place(key, near, first, back):
+        key = list(key)
+        for i in (range(n - 1, -1, -1) if back else range(n)):
+            for j, d in near[i]:
+                if key[j] >= key[i]:
+                    key[i] = key[j] + 1e-3
+        busy = {e: ([], []) for e in "vapgsx"}
+        start, pick = [0.0] * n, [None] * n
+        for i in sorted(range(n), key=lambda i: key[i]):
+            s0, h, got = first[i], hold[i], None
+            for j, d in near[i]:
+                if start[j] + d > s0:
+                    s0 = start[j] + d
+            for e in engs[i]:
+                a, b = busy[e]
+                s, m = s0, len(a)
+                k = m
+                while k and b[k - 1] > s:
+                    k -= 1
+                while k < m and s + h > a[k]:
+                    if b[k] > s:
+                        s = b[k]
+                    k += 1
+                if got is None or s <= got[0] + BIAS:
+                    got = (s, k, e)
+            s, k, e = got
+            pick[i], start[i] = e, s
+            busy[e][0].insert(k, s)
+            busy[e][1].insert(k, s + h)
+        return start, pick
+
+    def forward(key):
+        st, pk = place(key, fw, [0.0] * n, False)
+        return st, pk, max(st[i] + cost[i] for i in range(n))
+
+    late = [cost[i] - hold[i] for i in range(n)]
+    rest = list(cost)
+    for i in range(n - 1, -1, -1):
+        for j, d in fw[i]:
+            rest[j] = max(rest[j], d + rest[i])
+    best = cur = forward([-x for x in rest])
+    rnd = np.random.RandomState(SEED)
+    for it in range(TRIES):
+        c, w = rnd.rand() * best[2], 3000 + rnd.rand() * 12000
+        noise = ((rnd.rand(n) - 0.5) * NOISE).tolist()
+        key = [-(s + hold[i] + (noise[i] if abs(s - c) < w else 0.0)) for i, s in enumerate(cur[0])]
+        sb, _ = place(key, bw, late, True)
+        r = forward([-(sb[i] + hold[i]) for i in range(n)])
+        if r[2] <= cur[2] + SLACK * (1 - it / TRIES):
+            cur = r
+            if r[2] < best[2]:
+                best = r
+    st, pk, _ = best
+    return pre, st, [st[i] + cost[i] for i in range(n)], pk
+
+
+def close(ops, seq):
+    nxt = {}
+    for i in reversed(seq):
+        o = ops[i]
+        for x in o["r"] + o["w"]:
+            if x[0] in PSUM:
+                o["stop"] = nxt.get(x[0]) != "add"
+                nxt[x[0]] = o["cls"]
 
 
 def rank_program(g, core, T, topo):
@@ -527,6 +672,7 @@ def rank_program(g, core, T, topo):
         PLAN["plan"] = order(ops)
     pre, start, end, eng = PLAN["plan"]
     seq = sorted(range(len(ops)), key=lambda i: (start[i], i))
+    close(ops, seq)
     place = {i: k for k, i in enumerate(seq)}
     queue = {"v": g.vector, "a": g.scalar, "p": g.tensor, "g": g, "s": g.sync}
     need, marked, known = {}, set(), {e: {} for e in queue}

@@ -1,3 +1,4 @@
+import math
 import numpy as np
 from concourse.bass import DstId, RemoteDMATransfer
 from concourse.mybir import AluOpType, ActivationFunctionType
@@ -5,24 +6,25 @@ from concourse.mybir import AluOpType, ActivationFunctionType
 ALU = AluOpType
 ACT = ActivationFunctionType
 P, GH, NR, RO = 1024, 256, 6, 3
-B2, B0, GO, B1, END = 0, 1024, 2048, 3328, 4352
+G3, B2, B0, GO, B1, G2, TOP = 0, 256, 1280, 2304, 3584, 4608, 4864
 OWN = [B0, B1, B2]
-BASE = [B0, B0, B2]
-STOP = [B1, END, END]
-OFF = [1280, 1024]
+CAND = [GO, G2, G3]
+BASE = [B0, B0, G3]
+STOP = [B1, TOP, TOP]
+OFF = [1536, 512]
 BIG = 8192.0
 
 bf, f32, i32, u16, f16 = "bfloat16", "float32", "int32", "uint16", "float16"
 SCRATCH = {"MB": ("sbuf", [128, 16, 8, 16], bf)}
 for _dt, _list in (
-        (bf, "GX 8192 GY 8192 GZ 8192 GS 2048 W0 3328 W1 4352 W2 4352 UW 4352 FT 4352 DTa 2304 DTb 2304 HL 2304 RW 1024 VN 1024 MT 256 LT 1024 "
-             "DF0 1024 DF1 1024 DF2 1024 DF3 1024 DF4 1024 SG0 1024 SG1 1024 E 128 ID 128 LM 128 NL 128 PEN 128 EN 128 "
-             "ZB 144 ZK 144 ZH 144 ZA 144 ZC 144 ZP 144 ZM 144 EM 144 EP 144 CH 512 CN 96"),
-        (f32, "F 4352 FO 6144 X0 1024 X1 1024 X2 1024 TG0 256 TG1 256 TG2 256 TS0 256 TS1 256 TS2 256 TM 256 "
-              "COL 16 OH 4 GM 8 IL 64 KY 320 ZZ 320 AC 384"),
+        (bf, "GX 8192 GY 8192 GZ 8192 W0 3584 W1 4864 W2 4864 UW 4864 FT 4864 DTa 2304 DTb 2304 HL 2304 RW 1024 "
+             "VN 1024 MT 256 LT 1024 E 128 ID 128 LM 128 NL 128 PEN 128 EN 128 MS 128 "
+             "NG 128 ZB 144 ZK 144 ZG 144 ZH 144 ZA 144 ZC 144 ZP 144 ZM 144 EM 144 EP 144 CH 512 CM 512 CN 64"),
+        (f32, "F 4864 FO 9216 X0 1024 X1 1024 VP 1024 TG0 256 TG1 256 TG2 256 TS0 256 TS1 256 TS2 256 TM 256 "
+              "COL 16 OH 4 GM 8 IL 64 KY 320 ZZ 320 AC 64"),
         (i32, "SI 1024 AI 1024 IK 128 IK2 128 II 144 IZ 72 IM 64 IP 8 IO 4 GI 64 GJ 64 AJ 64 AK 64"),
         (u16, "HU0 512 HU1 512 CU 512 GL 64 KL 320 DR 64 D1 64 D2 64 LA 64 LB 64 FL 1024"),
-        (f16, "S16 1024 ZR 1152 I16 128 R0 144 R1 144 H0 512 H1 512 TT 512 CG 1024 B16 1024")):
+        (f16, "ZR 1152 I16 128 R0 144 R1 144 H0 512 H1 512 TT 512 C16 512 CG 1024 B16 1024 DG0 1024 DG1 1024 DG2 1024 SV 64")):
     _w = _list.split()
     for _k in range(0, len(_w), 2):
         SCRATCH[_w[_k]] = ("sbuf", [128, int(_w[_k + 1])], _dt)
@@ -32,16 +34,20 @@ for _k in PSUM:
 SEMAPHORES = (["cv", "ca", "cp", "cg"] + ["arV%d" % t for t in range(RO)] + ["arT%d" % t for t in range(RO)]
               + ["d%d" % k for k in range(80)])
 
-CG, CPE, LAT, OVH, CDMA, CREM = 1.55, 0.55, 150.0, 70.0, 2400.0, 4500.0
-TRIES, SEED, SLACK, NOISE = 12000, 3, 400.0, 3000.0
+CG, CPE, LAT, OVH, CDMA, CREM = 1.55, 0.5, 150.0, 70.0, 2400.0, 3000.0
+CASES = [(1.6, 1.1, 1.2, 0.35, 150.0), (1.2, 1.0, 1.0, 0.25, 150.0), (2.0, 1.2, 3.0, 0.4, 200.0)]
+ORDERS, SHAKES, MOVES, SEED, HEAT = 12, 250, 15000, 3, 100.0
 CHUNKS = [(0, 384), (384, 896), (896, 1024)]
 BANKS = [("A0", "B0"), ("A1", "B1"), ("P6", "P7")]
-CANDS = [(0, 512), (512, 1024)]
-GCH, XCH = 64, 64
-WAYS = ["aa", "vv", "aa", "vv", "va"]
+STEPS = ["k0", "k1", "c0", "c1", "k2", "c2"]
+CANDS = [(0, 1024)]
+GCH, XCH, YCH = 64, 128, 128
+WAYS = "avavv"
 KORD = [4, 0, 2, 1, 3]
-SLOTS = 6
-BIAS = 300.0
+KBANK = ["P6", "P4", "P7", "P6", "P4"]
+FIN = [2, 8, 14, 0, 4, 6, 10, 12, 5, 11, 1, 3, 7, 9, 13, 15]
+SLOTS = [("FO", P * _k) for _k in range(9)] + [("X0", 0), ("X1", 0), ("VP", 0)]
+KEEP = True
 PLAN = {}
 
 
@@ -51,7 +57,7 @@ def _conf(a, b):
 
 def build(g, core, T, topo):
     rank = T.rank_of(core)
-    ops = []
+    ops, sent = [], [None]
     V, S, PE = g.vector, g.scalar, g.tensor
 
     def reg(x):
@@ -103,6 +109,13 @@ def build(g, core, T, topo):
             return S.activation(ap(out), ap(in_), ACT.Identity, bias=add)
         return op("va", in_[2] - in_[1] + OVH, fn, [in_], [out])
 
+    def times(out, in_, mul, add=0.0):
+        def fn(e):
+            if e == "v":
+                return V.tensor_scalar(ap(out), ap(in_), mul, add, ALU.mult, ALU.add)
+            return S.activation(ap(out), ap(in_), ACT.Identity, bias=add, scale=mul)
+        return op("va", in_[2] - in_[1] + OVH, fn, [in_], [out])
+
     def gat(out, win, off, eng="va"):
         def fn(e):
             src = ap(win).indirect(ap(off))
@@ -137,8 +150,8 @@ def build(g, core, T, topo):
               for q in range(16)]
         r = [src, (z, 0, 144)]
         if tail is not None:
-            it.append((lo, lo + n // 16, T.ID[:, :], ap(tail), False))
-            r += [tail, ("ID", 0, 128)]
+            it.append((lo, lo + n // 16, T[tail[0]][:, :], ap(tail[1]), False))
+            r += [tail[1], (tail[0], 0, 128)]
         return mm(it, r, bank)
 
     def rowlist(bank, lo, o):
@@ -147,9 +160,9 @@ def build(g, core, T, topo):
         it = [(lo, lo + 64, T.ZR[:, z0 - 2 * u:z0 - 2 * u + 128], T[h][:, u:512:8], u == 0) for u in range(8)]
         return mm(it, [(h, 0, 512), ("ZR", 0, 1152)], bank)
 
-    def fold(e, src, n0, n1, lo, start):
+    def fold(e, src, n0, n1, lo):
         r = T["R%d" % e]
-        return [(lo, lo + (n1 - n0) // 2, r[:, 1 - h:129 - h], T[src][:, n0 + h:n1:2], start and h == 0) for h in range(2)]
+        return [(lo, lo + (n1 - n0) // 2, r[:, 1 - h:129 - h], T[src][:, n0 + h:n1:2], h == 0) for h in range(2)]
 
     def dma(out, in_, r, w, eng="s"):
         q = {"s": g.sync, "a": g.scalar}[eng]
@@ -158,12 +171,18 @@ def build(g, core, T, topo):
     def copy(out, in_):
         return dma(ap(out), ap(in_), [in_], [out])
 
+    def again(buf, src, t):
+        return copy((buf, CAND[t], CAND[t] + GH), (src, GO + GH * t, GO + GH * t + GH))
+
     def pool(out, n, pattern, base, cm, w, small=False):
         if small:
             fn = lambda e: g.iota(out, pattern, base, cm, allow_small_or_imprecise_dtypes=True)
         else:
             fn = lambda e: g.iota(out, pattern, base, cm)
-        return op("g", 2 * n + 160, fn, [], [w, ("pool", 0, 1)])
+        return op("g", 2 * n + 160, fn, [], [w, ("pool", 0, 1)], after=sent[0])
+
+    def count(buf, lo, hi, base):
+        return pool(T[buf][:, lo:hi], hi - lo, [[1, hi - lo]], base, 0, (buf, lo, hi), True)
 
     def fill(x, val):
         n = x[2] - x[1]
@@ -188,28 +207,33 @@ def build(g, core, T, topo):
 
     def send_values(t, src):
         dests = [(T.cores[(rank - d) % NR], T["W%d" % t][:, GO + (d - 1) * GH:GO + d * GH]) for d in range(1, NR)]
-        send(src, dests, "arV%d" % t, ("W%d" % t, GO, B1), CREM + 2500)
+        if t > 0:
+            sent[0] = len(ops)
+        send(src, dests, "arV%d" % t, ("W%d" % t, GO, B1), CREM + 4000)
 
     def send_tuples(t):
         send(("TS%d" % t, 0, 256), [(T.cores[(rank - t - 1) % NR], T["TG%d" % t][:, :])], "arT%d" % t,
-             ("TG%d" % t, 0, 256), CREM)
+             ("TG%d" % t, 0, 256), CREM + 1500)
 
     def col(k):
         return ("COL", k, k + 1)
+
+    def selves(t):
+        count("X%d" % (t % 2), 0, P, OWN[t] - B0 - OFF[(t + 1) % 2])
 
     dma(T.W0[:, B0:B0 + GH], T.v0[:, 0:GH], [], [("W0", B0, B0 + GH)])
     dma(T.SI[:, 0:GH], T.succ[:, 0:GH], [], [("SI", 0, GH)], eng="a")
     dma(T.W0[:, B0 + GH:GO], T.v0[:, GH:P], [], [("W0", B0 + GH, GO)])
     dma(T.SI[:, GH:P], T.succ[:, GH:P], [], [("SI", GH, P)], eng="a")
     dma(T.MT[:, :], T.mat[:, :], [], [("MT", 0, 256)])
-    dma(T.RW[:, :], T.rew[:, :], [], [("RW", 0, P)], eng="a")
+    dma(T.VN[:, :], T.rew[:, :], [], [("VN", 0, P)], eng="a")
     pool(T.II[:, :], 144, [[-1, 144]], 0, 1, ("II", 0, 144))
     pool(T.IP[:, 0:1], 1, [[0, 1]], 0, 1, ("IP", 0, 1))
     pool(T.IK[:, :], 128, [[-16, 8], [0, 16]], 0, 1, ("IK", 0, 128))
     pool(T.IM[:, :], 64, [[16, 64]], 0, 0, ("IM", 0, 64))
     send_values(0, ("W0", B0, B0 + GH))
     pool(T.IZ[:, :], 72, [[-2, 8], [-16, 9]], 0, 1, ("IZ", 0, 72))
-    pool(T.X0[:, :], P, [[1, P]], OWN[0] - B0 - OFF[1], 0, ("X0", 0, P), True)
+    selves(0)
 
     ts(("IP", 2, 3), ("IP", 0, 1), 15, None, ALU.bitwise_and)
     ts(("IP", 4, 5), ("IP", 0, 1), 1, None, ALU.bitwise_and)
@@ -220,14 +244,15 @@ def build(g, core, T, topo):
     for e in range(2):
         ts(("R%d" % e, 0, 144), ("II", 0, 144), float(e - 1), col(2 - e), ALU.is_equal, ALU.mult)
     for n0, n1 in ((0, GH), (GH, P)):
-        ts(("S16", n0, n1), ("SI", n0, n1), col(3), None, ALU.add)
+        ts(("DG0", n0, n1), ("SI", n0, n1), col(3), None, ALU.add)
         for e in range(2):
             bank = "P%d" % (4 + e)
-            mm(fold(e, "S16", n0, n1, n0 // 2, True), [("R%d" % e, 0, 144), ("S16", n0, n1)], bank)
+            mm(fold(e, "DG0", n0, n1, n0 // 2), [("R%d" % e, 0, 144), ("DG0", n0, n1)], bank)
             cp(("H%d" % e, n0 // 2, n1 // 2), (bank, n0 // 2, n1 // 2))
             ts(("HU%d" % e, n0 // 2, n1 // 2), ("H%d" % e, n0 // 2, n1 // 2), float(OFF[e]), None, ALU.add)
     ts(("TM", 0, 256), ("SI", 0, 256), float(GH), -BIG, ALU.is_ge, ALU.mult)
-    tt(("TS0", 0, 256), ("TM", 0, 256), ("SI", 0, 256), ALU.add)
+    tt(("TS1", 0, 256), ("TM", 0, 256), ("SI", 0, 256), ALU.add)
+    move(("TS0", 0, 256), ("TS1", 0, 256), float(CAND[0] - B0 - OFF[1]))
     send_tuples(0)
     ts(("IK2", 0, 128), ("IK", 0, 128), 4, None, ALU.arith_shift_right)
     ts(("E", 0, 128), ("IK2", 0, 128), 0.0, None, ALU.is_equal)
@@ -238,6 +263,9 @@ def build(g, core, T, topo):
     for a in range(8):
         fn = lambda e, a=a: S.activation(T.MB[:, :, a, :], T.MT[:, :], ACT.Identity, scale=T.GM[:, a:a + 1])
         op("a", 256 + OVH, fn, [("MT", 0, 256), ("GM", 0, 8)], [("MB", a, a + 1)])
+    act(("RW", 0, P), ("VN", 0, P), ACT.Identity, -128.0)
+    mm([(0, 128, T.ID[:, :], T.MB[:, o, :, :], o == 0) for o in range(16)], [("ID", 0, 128), ("MB", 0, 8)], "P6")
+    move(("MS", 0, 128), ("P6", 0, 128))
     ts(("IL", 0, 64), ("IM", 0, 64), col(0), None, ALU.add)
     fill(("ZB", 0, 144), 0.0)
     op("v", 64 + OVH, lambda e: V.tensor_copy(T.ZB[:, 15:143:16], T.E[:, 0:128:16]), [("E", 0, 128)], [("ZB", 0, 144)])
@@ -245,7 +273,9 @@ def build(g, core, T, topo):
     for h in range(2):
         op("v", 72 + OVH, lambda e, h=h: V.tensor_scalar(T.ZR[:, 14 + h:1152:16], T.IZ[:, :], float(h), None, ALU.is_equal),
            [("IZ", 0, 72)], [("ZR", 0, 1152)])
-    ts(("ZK", 0, 144), ("ZB", 0, 144), 65536.0, None, ALU.mult)
+    times(("ZK", 0, 144), ("ZB", 0, 144), 65536.0)
+    times(("ZG", 0, 144), ("ZB", 0, 144), 1048576.0)
+    times(("NG", 0, 128), ("ID", 0, 128), -1048576.0)
     ts(("IO", 0, 4), ("II", 0, 4), 15, None, ALU.bitwise_and)
     ts(("OH", 0, 4), ("IO", 0, 4), 0.0, None, ALU.is_equal)
     ts(col(4), ("OH", 0, 1), 64.0, ("OH", 1, 2), ALU.mult, ALU.add)
@@ -258,31 +288,29 @@ def build(g, core, T, topo):
         fill((z, 0, 144), 0.0)
         op("v", 64 + OVH, lambda e, z=z, wt=wt: V.tensor_scalar(T[z][:, 1:129:2], T.E[:, 0:128:2], wt, None, ALU.mult),
            [("E", 0, 128)], [(z, 0, 144)])
-    ts(("PEN", 0, 128), ("E", 0, 128), -BIG, None, ALU.mult)
-    ts(("NL", 0, 128), ("ID", 0, 128), 4096.0, None, ALU.mult)
+    times(("PEN", 0, 128), ("E", 0, 128), -BIG)
+    times(("NL", 0, 128), ("ID", 0, 128), 4096.0)
     tt(("LM", 0, 128), ("NL", 0, 128), ("E", 0, 128), ALU.max)
-    ts(("NL", 0, 128), ("LM", 0, 128), -1.0, None, ALU.mult)
-    fill(("CH", 0, 512), -1152.0)
-    fill(("CN", 0, 32), 0.0)
-    fill(("CN", 32, 96), -983040.0)
+    times(("NL", 0, 128), ("LM", 0, 128), -1.0)
+    fill(("CH", 0, 512), -1280.0)
+    fill(("CM", 0, 512), 128.0)
+    times(("CN", 0, 64), ("E", 0, 64), 0.0, -983040.0)
     pool(T.HL[0:32, :], 2304, [[1, 36], [0, 64]], 0, 0, ("HL", 0, 2304, 0), True)
     pool(T.HL[32:64, :], 2304, [[0, 36], [1, 64]], 0, 0, ("HL", 0, 2304, 1), True)
     for r, cut in ((2, GH), (3, P)):
         pool(T.HL[32 * r:32 * r + 32, 0:cut], cut, [[0, cut]], 0, 0, ("HL", 0, cut, r), True)
         pool(T.HL[32 * r:32 * r + 32, cut:2304], 2304 - cut, [[0, 2304 - cut]], 1, 0, ("HL", cut, 2304, r), True)
-    pool(T.X1[:, :], P, [[1, P]], OWN[1] - B0 - OFF[0], 0, ("X1", 0, P), True)
-    pool(T.X2[:, :], P, [[1, P]], OWN[2] - B0 - OFF[1], 0, ("X2", 0, P), True)
-    pool(T.F[:, GO:B1], B1 - GO, [[1, B1 - GO]], P, 0, ("F", GO, B1), True)
     for r in range(4):
         dma(T.FT[r:128:4, B0:B1], T.HL[32 * r:32 * r + 32, :], [("HL", 0, 2304, r)], [("FT", B0, B1, r)])
     copy(("DTa", P, 2304), ("FT", GO, B1))
     copy(("DTb", P, 2304), ("FT", GO, B1))
-    copy(("FT", B1, END), ("FT", B0, GO))
+    copy(("FT", B1, G2), ("FT", B0, GO))
     copy(("FT", B2, B0), ("FT", B0, GO))
+    again("FT", "FT", 1)
+    again("FT", "FT", 2)
     copy(("W2", B0, GO), ("W0", B0, GO))
 
-    def guests(src):
-        tolist("P7", 0, "ZB", src)
+    def guests():
         tt(("GI", 0, 64), ("P7", 0, 64), ("IL", 0, 64), ALU.add)
         ts(("GJ", 0, 64), ("GI", 0, 64), GH - 1, None, ALU.bitwise_and)
         cp(("GL", 0, 64), ("GJ", 0, 64))
@@ -297,12 +325,9 @@ def build(g, core, T, topo):
                 k = o // 3
                 act(("KY", 64 * k, 64 * k + 64), (bank, 64 * j, 64 * j + 64), ACT.Identity, off + 8192.0 * (5 - k))
 
-    FIN = [2, 8, 14, 0, 4, 6, 10, 12, 5, 11, 1, 3, 7, 9, 13, 15]
-
     def klist(t, k):
         if t + 1 < RO:
-            c = 64 * [0, 3, 1, 4, 2][k]
-            return "KL", c
+            return "KL", 64 * [0, 3, 1, 4, 2][k]
         return "FL", 64 * FIN.index(3 * k + t)
 
     def early(t):
@@ -310,21 +335,27 @@ def build(g, core, T, topo):
 
     def compose(buf, t):
         if t == 2:
-            gat2((buf, B1, END), (buf, B2, B1), ("LB", 0, 64))
+            gat2((buf, B1, G2), (buf, B2, B1), ("LB", 0, 64))
         if t >= 1:
-            gat2((buf, B0, GO), (buf, GO, END), ("LA", 0, 64))
+            gat2((buf, B0, GO), (buf, GO, G2), ("LA", 0, 64))
 
     def one_round(t):
-        W, X, TG = "W%d" % t, "X%d" % t, "TG%d" % t
+        W, X, TG = "W%d" % t, "X%d" % (t % 2), "TG%d" % t
         par = (t + 1) % 2
         own = OWN[t]
         H, HU = "H%d" % par, "HU%d" % par
-        copy(("UW", GO, B1), (W, GO, B1))
-        vb, v0 = ("W%d" % (t + 1), OWN[t + 1]) if t + 1 < RO else ("VN", 0)
+        if t == 0:
+            for lo in range(GO, B1, 640):
+                act(("UW", lo, lo + 640), (W, lo, lo + 640), ACT.Identity, -128.0)
+        else:
+            copy(("UW", GO, B1), (W, GO, B1))
+            for u in range(1, t + 1):
+                again(W, W, u)
+                again("UW", W, u)
 
-        def arcs(buf, lst, win, e, n0, n1, banks, ch):
-            ch = min(ch, (n1 - n0) // 2)
-            for c0 in range(n0 // 2, n1 // 2, ch):
+        def arcs(buf, lst, win, e, n0, n1, banks, most):
+            for c0 in range(n0 // 2, n1 // 2, most):
+                ch = min(most, n1 // 2 - c0)
                 x = (buf, 16 * c0, 16 * (c0 + ch))
                 gat(x, win, (lst, c0, c0 + ch))
                 lo = 2 * c0 - n0
@@ -335,50 +366,69 @@ def build(g, core, T, topo):
         def kept(j):
             n0, n1 = CHUNKS[j]
             for bank in BANKS[j]:
-                mm([(0, n1 - n0, T.ID[:, :], T.RW[:, n0:n1], True)], [("ID", 0, 128), ("RW", n0, n1)], bank)
-            arcs("GX", "HU%d" % (1 - par), (W, B0, STOP[t]), 1 - par, n0, n1, BANKS[j], XCH)
-            arcs("GY", HU, (W, B0, STOP[t]), par, n0, n1, BANKS[j][:1], GCH)
-            ts(("AI", n0, n1), (BANKS[j][0], 0, n1 - n0), 255.25, -255.0 / 512, ALU.min, ALU.add)
+                it = [(0, n1 - n0, T.ID[:, :], T.RW[:, n0:n1], True)]
+                if t > 0:
+                    it.append((0, n1 - n0, T.MS[:, :], T.CM[:, 0:n1 - n0], False))
+                mm(it, [("ID", 0, 128), ("RW", n0, n1), ("MS", 0, 128), ("CM", 0, 512)][:2 * len(it)], bank)
+            arcs("GX", "HU%d" % (1 - par), (W, B0, TOP if t == 2 else B1), 1 - par, n0, n1, BANKS[j], XCH)
+            arcs("GY", HU, (W, B0, B1), par, n0, n1, BANKS[j][:1], YCH)
+            ts(("AI", n0, n1), (BANKS[j][0], 0, n1 - n0), 127.25, -255.0 / 512, ALU.min, ALU.add)
+
+        cw = [(B0, B1), (B1, TOP), (G3, B0)][t]
 
         def cands(j):
             n0, n1 = CANDS[j]
-            gtt(("CG", n0, n1), (TG, 0, 256), ("GL", n0 // 16, n1 // 16), (X, n0, n1), ALU.min if t == 1 else ALU.max)
-            mm(fold(par, "CG", n0, n1, n0 // 2, True), [("R%d" % par, 0, 144), ("CG", n0, n1)], "P5")
-            ts(("CU", n0 // 2, n1 // 2), ("P5", n0 // 2, n1 // 2), float(OFF[par] + B0 - BASE[t]), None, ALU.add)
+            gtt(("CG", n0, n1), (TG, 0, 256), ("GL", n0 // 16, n1 // 16), (X, n0, n1), ALU.min if t == 2 else ALU.max)
+            mm(fold(par, "CG", n0, n1, n0 // 2), [("R%d" % par, 0, 144), ("CG", n0, n1)], "P5")
+            if KEEP:
+                cp(("C16", n0 // 2, n1 // 2), ("P5", n0 // 2, n1 // 2))
+            ts(("CU", n0 // 2, n1 // 2), ("C16" if KEEP else "P5", n0 // 2, n1 // 2), float(OFF[par] + B0 - cw[0]), None, ALU.add)
 
         def choose(j):
             n0, n1 = CHUNKS[j]
             w, x, y = n1 - n0, n0 // 2, n1 // 2
             a, b = BANKS[j]
-            arcs("GZ", "CU", (W, BASE[t], B1 if t == 2 else STOP[t]), par, n0, n1, [b], GCH)
+            arcs("GZ", "CU", (W, cw[0], cw[1]), par, n0, n1, [b], GCH)
             mm([(0, w, T.ID[:, :], T.CH[:, 0:w], True)], [("ID", 0, 128), ("CH", 0, 512)], a)
             tt(("LT", n0, n1), (b, 0, w), ("AI", n0, n1), ALU.is_lt)
-            ts(("B16", n0, n1), (b, 0, w), 255.25, 1152 - 255.0 / 512, ALU.min, ALU.add)
+            ts(("B16", n0, n1), (b, 0, w), 127.25, 1280 - 255.0 / 512, ALU.min, ALU.add)
             mm([(0, w, T.PEN[:, :], T.LT[:, n0:n1], False)], [("PEN", 0, 128), ("LT", n0, n1)], a)
             mm([(0, w, T.I16[:, :], T.B16[:, n0:n1], False)], [("I16", 0, 128), ("B16", n0, n1)], a)
-            tt(("UW", own + n0, own + n1), (a, 0, w), ("AI", n0, n1), ALU.max)
-            if t + 1 < RO:
+            vc = ("UW", own + n0, own + n1)
+            tt(vc, (a, 0, w), ("AI", n0, n1), ALU.max)
+            move(("VP", n0, n1), vc, 1.0 / 16)
+            if t + 1 == RO:
+                move(("VN", n0, n1), vc, 128.0)
+                dma(T.yv[:, n0:n1], T.VN[:, n0:n1], [("VN", n0, n1)], [])
+            else:
                 if n0 == 0:
                     send_values(t + 1, ("UW", own, own + GH))
-            (copy if n1 < P else cp)((vb, v0 + n0, v0 + n1), ("UW", own + n0, own + n1))
-            if t + 1 == RO:
-                dma(T.yv[:, n0:n1], T.UW[:, own + n0:own + n1], [("UW", own + n0, own + n1)], [])
-            for lo, z in ((0, "EM"), (256, "EP")):
-                it = fold(par, "CG", n0, n1, lo, True)
-                it += [(lo, lo + w // 2, T[z][:, 1 - h:129 - h], T.LT[:, n0 + h:n1:2], False) for h in range(2)]
-                mm(it, [("R%d" % par, 0, 144), ("CG", n0, n1), (z, 0, 144), ("LT", n0, n1)], b)
-            tt(("TT", x, y), (b, 0, w // 2), (H, x, y), ALU.max)
-            tt((H, x, y), (b, 256, 256 + w // 2), ("TT", x, y), ALU.min)
+                    selves(t + 1)
+                    if t == 0:
+                        count("F", GO, B1, P)
+                        count("F", G2, TOP, P + GH)
+                        count("F", G3, B2, P + 2 * GH)
+                copy(("W%d" % (t + 1), OWN[t + 1] + n0, OWN[t + 1] + n1), vc)
+            steps = [[("EM", "TT", H, ALU.max), ("EP", H, "TT", ALU.min)], [("EM", H, H, ALU.max)], [("EP", H, H, ALU.min)]][t]
+            for u, (z, _, _, _) in enumerate(steps):
+                it = fold(par, "CG", n0, n1, 256 * u)
+                if KEEP:
+                    it = [(256 * u, 256 * u + w // 2, T.I16[:, :], T.C16[:, x:y], True)]
+                it += [(256 * u, 256 * u + w // 2, T[z][:, 1 - h:129 - h], T.LT[:, n0 + h:n1:2], False) for h in range(2)]
+                mm(it, [("R%d" % par, 0, 144), ("C16", x, y) if KEEP else ("CG", n0, n1), (z, 0, 144), ("LT", n0, n1)], b)
+            for u, (_, out, in1, o) in enumerate(steps):
+                tt((out, x, y), (b, 256 * u, 256 * u + w // 2), (in1, x, y), o)
             if t + 1 < RO:
                 ts((HU, x, y), (H, x, y), float(OFF[par]), None, ALU.add)
 
         for j in range(len(CANDS)):
             cands(j)
-        for j in range(len(CHUNKS)):
-            kept(j)
-        for j in range(len(CHUNKS)):
-            choose(j)
-        vn = ("UW", own, own + P)
+        for step in STEPS:
+            (kept if step[0] == "k" else choose)(int(step[1]))
+        tolist("P7", 0, "ZB", ("UW", own, own + P))
+        cp(("SV", 0, 64), ("P7", 0, 64))
+        if t + 1 < RO:
+            guests()
         compose("UW", t)
         lists(t, [t + 3, t + 9], "P5", ("KL", 192) if t + 1 < RO else ("FL", 512))
         acc = ("IL", 0, 64)
@@ -387,27 +437,25 @@ def build(g, core, T, topo):
             act(acc, ("IL", 0, 64), ACT.Identity, float(own - BASE[t]))
         uw = ("UW", BASE[t], STOP[t])
         for j, k in enumerate(KORD):
-            df, bank, c, way = "DF%d" % k, ("P7" if j % 2 == 0 else "P6"), 64 * (k + 1), WAYS[k]
+            bank, c, way = KBANK[j], 128 + 64 * k, WAYS[k]
             kb, kc = klist(t, k)
-            for b in range(2):
-                lo, hi, bk = 512 * b, 512 * b + 512, ("A%d" if k == 0 else "B%d") % b
-                kl = (kb, kc + 32 * b, kc + 32 * b + 32)
-                if way[b] == "a":
-                    sg = "SG%d" % (j % 2)
-                    gat((sg, lo, hi), uw, kl, eng="a")
-                    mm([(0, 512, T.NL[:, :], T.UW[:, own + lo:own + hi], True),
-                        (0, 512, T.LM[:, :], T[sg][:, lo:hi], False)],
-                       [("NL", 0, 128), ("LM", 0, 128), ("UW", own + lo, own + hi), (sg, lo, hi)], bk)
-                    act((df, lo, hi), (bk, 0, 512), ACT.Sign, -0.5)
-                elif way == "vv" and b == 0:
-                    gtt((df, 0, P), uw, (kb, kc, kc + 64), (vb, v0, v0 + P), ALU.subtract)
-                    ts((df, 0, P), (df, 0, P), 16.0, 1.0, ALU.mult, ALU.min)
-                elif way != "vv":
-                    gtt((df, lo, hi), uw, kl, (vb, v0 + lo, v0 + hi), ALU.subtract)
-                    ts((df, lo, hi), (df, lo, hi), 16.0, 1.0, ALU.mult, ALU.min)
-            tolist(bank, c, "ZK", (df, 0, P), tail={"aa": ("CN", 32, 96), "va": ("CN", 0, 64), "vv": None}[way])
+            u = WAYS[:k].count(way)
+            if way == "a":
+                df, sg = 2048 + P * u, P * u
+                for lo in (0, 512):
+                    hi, bk = lo + 512, ("A0", "A1", "B0", "B1")[2 * u + lo // 512]
+                    mm([(0, 512, T.NL[:, :], T.UW[:, own + lo:own + hi], True)], [("NL", 0, 128), ("UW", own + lo, own + hi)], bk)
+                    x = ("GZ", sg + lo, sg + hi)
+                    gat(x, uw, (kb, kc + lo // 16, kc + hi // 16), eng="a")
+                    mm([(0, 512, T.LM[:, :], ap(x), False)], [("LM", 0, 128), x], bk)
+                    act(("GZ", df + lo, df + hi), (bk, 0, 512), ACT.Sign, -0.5)
+                tolist(bank, c, "ZK", ("GZ", df, df + P), tail=("ID", ("CN", 0, 64)))
+            else:
+                df = "DG%d" % u
+                gtt((df, 0, P), uw, (kb, kc, kc + 64), ("VP", 0, P), ALU.min)
+                tolist(bank, c, "ZG", (df, 0, P), tail=("NG", ("SV", 0, 64)))
             tt(("ZZ", 64 * k, 64 * k + 64), (bank, c, c + 64), ("KY", 64 * k, 64 * k + 64), ALU.min)
-            nxt = ("AJ", 0, 64) if j == 4 else ("AC", 64 * j + 64, 64 * j + 128)
+            nxt = ("AJ", 0, 64) if j == 4 else ("P5", 448, 512)
             tt(nxt, acc, ("ZZ", 64 * k, 64 * k + 64), ALU.max)
             acc = nxt
         ts(("AK", 0, 64), ("AJ", 0, 64), 8191, None, ALU.bitwise_and)
@@ -419,7 +467,6 @@ def build(g, core, T, topo):
             d1 = ("D1", 0, 64)
             cp(d1, ("P6", 448, 512))
         if t + 1 < RO:
-            guests(vn)
             early(t + 1)
         else:
             lists(t, FIN[3:8], "P4", ("FL", 192))
@@ -435,17 +482,17 @@ def build(g, core, T, topo):
             else:
                 tolist("P7", 448, "ZC", ("FT", own, own + P))
                 cp(("LB", 0, 64), ("P7", 448, 512))
-                gat2(("FT", B0, GO), ("FT", GO, END), ("LA", 0, 64))
+                gat2(("FT", B0, GO), ("FT", GO, G2), ("LA", 0, 64))
             compose("W%d" % (t + 1), t + 1)
             for h in range(2):
-                gat(("GS", P * h, P * h + P), ("FT", B0, B1), ("HU%d" % (1 - par), 64 * h, 64 * h + 64))
-            z = "ZP" if t == 0 else "ZM"
+                gat(("GZ", 4096 + P * h, 5120 + P * h), ("FT", B0, B1), ("HU%d" % (1 - par), 64 * h, 64 * h + 64))
+            z = "ZM" if t == 0 else "ZP"
             it = []
             for s in range(16):
                 o = s - s % 2 + 1 - par
-                it.append((64 + s % 2, 320, T[z][:, 15 - o:143 - o], T.GS[:, s:2048:16], s == 0))
-            mm(it, [(z, 0, 144), ("GS", 0, 2048)], "P7", step=2)
-            move(("TS%d" % (t + 1), 0, 256), ("P7", 64, 320), float(P + GH * (t + 1) - OFF[1 - par]))
+                it.append((64 + s % 2, 320, T[z][:, 15 - o:143 - o], T.GZ[:, 4096 + s:6144:16], s == 0))
+            mm(it, [(z, 0, 144), ("GZ", 4096, 6144)], "P7", step=2)
+            move(("TS%d" % (t + 1), 0, 256), ("P7", 64, 320), float(CAND[t + 1] - B0 - OFF[1 - par]))
             send_tuples(t + 1)
         else:
             for b in range(2):
@@ -455,116 +502,21 @@ def build(g, core, T, topo):
             gat2(("F", B2, B0), ("F", B0, B1), ("D2", 0, 64))
             compose("F", t)
 
-    guests(("W0", B0, GO))
+    tolist("P7", 0, "ZB", ("W0", B0, GO))
+    guests()
     early(0)
     for t in range(RO):
         one_round(t)
     for j, o in enumerate(FIN):
-        s = P * (j % SLOTS)
+        buf, s = SLOTS[j % len(SLOTS)]
         for lo, hi in ((0, P),) if j < 14 else ((0, 512), (512, P)):
-            gat(("FO", s + lo, s + hi), ("F", B2, END), ("FL", 64 * j + lo // 16, 64 * j + hi // 16))
-            dma(T.ys[o:128:16, lo:hi], T.FO[0:128:16, s + lo:s + hi], [("FO", s + lo, s + hi)], [])
+            gat((buf, s + lo, s + hi), ("F", G3, TOP), ("FL", 64 * j + lo // 16, 64 * j + hi // 16))
+            dma(T.ys[o:128:16, lo:hi], T[buf][0:128:16, s + lo:s + hi], [(buf, s + lo, s + hi)], [])
     return ops
 
 
-def order(ops):
-    n = len(ops)
-    pre = [set() for _ in range(n)]
-    seen = {}
-    for i, o in enumerate(ops):
-        if o["after"] is not None:
-            pre[i].add(o["after"])
-        for x, wr in [(x, False) for x in o["r"]] + [(x, True) for x in o["w"]]:
-            lst = seen.setdefault(x[0], [])
-            for j, y, wy in (lst[-1:] if x[0] in PSUM else lst):
-                if x[0] in PSUM or ((wr or wy) and _conf(x, y)):
-                    pre[i].add(j)
-        for x in o["r"]:
-            seen[x[0]].append((i, x, False))
-        for x in o["w"]:
-            seen[x[0]].append((i, x, True))
-    pre = [sorted(x) for x in pre]
-    cost = [o["cost"] for o in ops]
-    hold = [{"c": o["cost"], "d": 100.0, "r": 600.0, "x": 0.0}[o["kind"]] for o in ops]
-    near = [[(j, 0.0 if ops[i]["eng"] == "p" and ops[j]["eng"] == "p" else LAT) for j in pre[i]] for i in range(n)]
-
-    def place(key, pick):
-        key = list(key)
-        pick = list(pick)
-        for i in range(n):
-            for j in pre[i]:
-                if key[j] >= key[i]:
-                    key[i] = key[j] + 1e-4
-        busy = {e: [] for e in "vapgsx"}
-        start, end, why = [0.0] * n, [0.0] * n, [-1] * n
-        for i in sorted(range(n), key=lambda i: key[i]):
-            s0, w0 = 0.0, -1
-            for j, d in near[i]:
-                if end[j] + d > s0:
-                    s0, w0 = end[j] + d, j
-            got = None
-            for e in pick[i]:
-                s, w, q = s0, w0, busy[e]
-                k = len(q)
-                while k and q[k - 1][1] > s:
-                    k -= 1
-                while k < len(q) and s + hold[i] > q[k][0]:
-                    if q[k][1] > s:
-                        s, w = q[k][1], q[k][2]
-                    k += 1
-                if got is None or s <= got[0]:
-                    got = (s, w, k, e)
-            s, w, k, pick[i] = got
-            busy[pick[i]].insert(k, (s, s + hold[i], i))
-            start[i], end[i], why[i] = s, s + cost[i], w
-        return (start, end, why), pick
-
-    rest = list(cost)
-    for i in range(n - 1, -1, -1):
-        for j, d in near[i]:
-            rest[j] = max(rest[j], cost[j] + d + rest[i])
-    res, pick = place([-x for x in rest], [o["eng"] for o in ops])
-    best = (res, pick)
-    x = SEED
-    for it in range(TRIES):
-        i = max(range(n), key=lambda i: res[1][i])
-        pairs = []
-        while res[2][i] >= 0:
-            j = res[2][i]
-            if j not in pre[i]:
-                pairs.append((j, i))
-            i = j
-        x = (x * 1103515245 + 12345) % 2147483648
-        j, i = pairs[(x >> 8) % len(pairs)]
-        x = (x * 1103515245 + 12345) % 2147483648
-        how = (x >> 12) % 5
-        key, p2 = list(res[0]), list(pick)
-        if how == 0 and len(ops[i]["eng"]) > 1:
-            p2[i] = "a" if p2[i] == "v" else "v"
-        elif how == 1 and len(ops[j]["eng"]) > 1:
-            p2[j] = "a" if p2[j] == "v" else "v"
-        elif how == 2:
-            key[j] = key[i] + (x >> 16) % 2000
-        else:
-            key[i] = key[j] - 1 - ((x >> 16) % 3000 if how == 3 else 0)
-            stack = [i]
-            while stack:
-                a = stack.pop()
-                for b in pre[a]:
-                    if key[b] >= key[a]:
-                        key[b] = key[a] - 1e-3
-                        stack.append(b)
-        r2, p2 = place(key, p2)
-        if max(r2[1]) <= max(res[1]) + SLACK * (1 - it / TRIES):
-            res, pick = r2, p2
-            if max(res[1]) < max(best[0][1]):
-                best = (res, pick)
-    return pre, best[0][0], best[0][1], best[1]
-
-
-def order(ops):
-    n = len(ops)
-    pre = [set() for _ in range(n)]
+def needs(ops):
+    pre = [set() for _ in ops]
     seen = {}
     for i, o in enumerate(ops):
         if o["after"] is not None:
@@ -586,17 +538,62 @@ def order(ops):
             seen[x[0]].append((i, x, False))
         for x in o["w"]:
             seen[x[0]].append((i, x, True))
-    pre = [sorted(x) for x in pre]
-    cost = [o["cost"] for o in ops]
-    hold = [{"c": o["cost"], "d": 100.0, "r": 600.0, "x": 0.0}[o["kind"]] for o in ops]
+    return [sorted(x) for x in pre]
+
+
+def behind(ops, i, j):
+    return ops[i]["kind"] == "c" and ops[i]["after"] == j
+
+
+def plan(ops):
+    made = [order(ops, SEED + k, MOVES, HEAT) for k in range(ORDERS)]
+    cuts = [i for i, o in enumerate(ops) if o["w"] and o["w"][0][0] == "DR"]
+
+    def join(which):
+        seq, pick, done = [], [None] * len(ops), set()
+        for s, k in enumerate(which):
+            other = made[k][1]
+            for i in other[:other.index(cuts[s]) + 1] if s < len(cuts) else other:
+                if i not in done:
+                    done.add(i)
+                    seq.append(i)
+                    pick[i] = made[k][2][i]
+        return order(ops, SEED, 0, HEAT, (seq, pick))
+
+    which = [min(range(ORDERS), key=lambda k: made[k][4])] * (len(cuts) + 1)
+    best = join(which)
+    for s in range(len(which)):
+        for k in range(ORDERS):
+            w2 = which[:s] + [k] + which[s + 1:]
+            r = join(w2)
+            if r[4] < best[4]:
+                which, best = w2, r
+    return order(ops, SEED, MOVES, HEAT / 2, (best[1], best[2]))
+
+
+def order(ops, seed, moves, heat, given=None):
+    n = len(ops)
+    pre = needs(ops)
     engs = [o["eng"] for o in ops]
-    fw = [[] for _ in range(n)]
-    bw = [[] for _ in range(n)]
+    suc = [[] for _ in range(n)]
     for i in range(n):
         for j in pre[i]:
-            d = 0.0 if engs[i] == "p" and engs[j] == "p" else LAT
-            fw[i].append((j, d + cost[j]))
-            bw[j].append((i, d + hold[i] + cost[j] - hold[j]))
+            suc[j].append(i)
+
+    def case(cg, near, far, lat):
+        cost = [(o["cost"] - OVH) * cg / CG + OVH if o["cls"] == "g" else
+                {"d": o["cost"] * near, "r": CREM * near + (o["cost"] - CREM) * far}.get(o["kind"], o["cost"]) for o in ops]
+        hold = [{"c": c, "d": 1200.0 if o["eng"] == "g" else 100.0, "r": 600.0, "x": 0.0}[o["kind"]] for o, c in zip(ops, cost)]
+        near = [[(j, hold[j] if behind(ops, i, j) else cost[j] + (0.0 if engs[i] == "p" and engs[j] == "p" else lat))
+                 for j in pre[i]] for i in range(n)]
+        return cost, hold, near
+
+    cases = [case(c[0], c[1], c[2], c[4]) for c in CASES]
+    cost, hold, fw = cases[0]
+    bw = [[] for _ in range(n)]
+    for i in range(n):
+        for j, d in fw[i]:
+            bw[j].append((i, d + hold[i] - hold[j]))
 
     def place(key, near, first, back):
         key = list(key)
@@ -621,7 +618,7 @@ def order(ops):
                     if b[k] > s:
                         s = b[k]
                     k += 1
-                if got is None or s <= got[0] + BIAS:
+                if got is None or s <= got[0] + 300.0:
                     got = (s, k, e)
             s, k, e = got
             pick[i], start[i] = e, s
@@ -634,24 +631,110 @@ def order(ops):
         return st, pk, max(st[i] + cost[i] for i in range(n))
 
     late = [cost[i] - hold[i] for i in range(n)]
-    rest = list(cost)
-    for i in range(n - 1, -1, -1):
-        for j, d in fw[i]:
-            rest[j] = max(rest[j], d + rest[i])
-    best = cur = forward([-x for x in rest])
-    rnd = np.random.RandomState(SEED)
-    for it in range(TRIES):
+    best = cur = forward(range(n))
+    rnd = np.random.RandomState(seed)
+    for it in range(0 if given else SHAKES):
         c, w = rnd.rand() * best[2], 3000 + rnd.rand() * 12000
-        noise = ((rnd.rand(n) - 0.5) * NOISE).tolist()
+        noise = ((rnd.rand(n) - 0.5) * 3000).tolist()
         key = [-(s + hold[i] + (noise[i] if abs(s - c) < w else 0.0)) for i, s in enumerate(cur[0])]
         sb, _ = place(key, bw, late, True)
         r = forward([-(sb[i] + hold[i]) for i in range(n)])
-        if r[2] <= cur[2] + SLACK * (1 - it / TRIES):
+        if r[2] <= cur[2] + 400.0 * (1 - it / SHAKES):
             cur = r
             if r[2] < best[2]:
                 best = r
-    st, pk, _ = best
-    return pre, st, [st[i] + cost[i] for i in range(n)], pk
+
+    def replay(seq, pick, cs, old, a):
+        cost, hold, near = cs
+        free, last = dict.fromkeys("vapgsx", 0.0), dict.fromkeys("vapgsx", -1)
+        start, why = list(old[1]), list(old[2])
+        todo = 5
+        for k in range(a - 1, -1, -1):
+            i = seq[k]
+            e = pick[i]
+            if last[e] < 0 and e != "x":
+                free[e], last[e] = start[i] + hold[i], i
+                todo -= 1
+                if not todo:
+                    break
+        top, ti = 0.0, -1
+        for i in seq[a:]:
+            e = pick[i]
+            t, w = free[e], last[e]
+            for j, d in near[i]:
+                if start[j] + d > t:
+                    t, w = start[j] + d, j
+            start[i], why[i] = t, w
+            if e != "x":
+                free[e], last[e] = t + hold[i], i
+            if t + cost[i] > top:
+                top, ti = t + cost[i], i
+        return top, start, why, ti
+
+    def score(seq, pick, old, a):
+        rs = [replay(seq, pick, cs, r, min(a, n - 40)) for cs, r in zip(cases, old)]
+        return sum(r[0] * c[3] for r, c in zip(rs, CASES)), rs
+
+    seq, pick = given or (sorted(range(n), key=lambda i: (best[0][i], i)), best[1])
+    cur, rs = score(seq, pick, [(0, [0.0] * n, [-1] * n)] * len(cases), 0)
+    best = (cur, seq, pick, rs)
+    either = [m for m in range(n) if len(engs[m]) > 1]
+    for it in range(moves):
+        r = rs[rnd.randint(len(rs))]
+        i, pairs = r[3], []
+        while r[2][i] >= 0:
+            j = r[2][i]
+            if j not in pre[i]:
+                pairs.append((j, i))
+            i = j
+        j, i = pairs[rnd.randint(len(pairs))]
+        how = rnd.randint(6)
+        s2, p2 = seq, pick
+        if how < 2:
+            k = (i, j)[how]
+            if len(engs[k]) < 2:
+                continue
+            p2 = list(pick)
+            p2[k] = "a" if p2[k] == "v" else "v"
+            a = seq.index(k)
+            if rnd.rand() < 0.5:
+                c = [m for m in either if pick[m] == p2[k] and abs(r[1][m] - r[1][k]) < 4000]
+                if c:
+                    m = c[rnd.randint(len(c))]
+                    p2[m] = pick[k]
+                    a = min(a, seq.index(m))
+        else:
+            a, b = seq.index(j), seq.index(i)
+            if how < 4:
+                a = max(0, a - (rnd.randint(30) if how == 3 else 0))
+                need, mv = set(pre[i]), [i]
+                for m in reversed(seq[a:b]):
+                    if m in need:
+                        mv.append(m)
+                        need.update(pre[m])
+                ms = set(mv)
+                s2 = seq[:a] + mv[::-1] + [m for m in seq[a:b] if m not in ms] + seq[b + 1:]
+            else:
+                b = min(n - 1, b + (rnd.randint(30) if how == 5 else 0))
+                need, mv = set(suc[j]), [j]
+                for m in seq[a + 1:b + 1]:
+                    if m in need:
+                        mv.append(m)
+                        need.update(suc[m])
+                ms = set(mv)
+                s2 = seq[:a] + [m for m in seq[a + 1:b + 1] if m not in ms] + mv + seq[b + 1:]
+        room = -math.log(1.0 - rnd.rand()) * (heat * (1 - it / moves) + 1)
+        c2, r2 = 0.0, []
+        for cs, r, c in zip(cases, rs, CASES):
+            r2.append(replay(s2, p2, cs, r, min(a, n - 40)))
+            c2 += (r2[-1][0] - r[0]) * c[3]
+            if c2 > room + 150.0:
+                break
+        if c2 <= room:
+            seq, pick, cur, rs = s2, p2, cur + c2, r2
+            if cur < best[0]:
+                best = (cur, seq, pick, rs)
+    return pre, best[1], best[2], best[3], best[0]
 
 
 def close(ops, seq):
@@ -669,9 +752,8 @@ def rank_program(g, core, T, topo):
         return
     ops = build(g, core, T, topo)
     if "plan" not in PLAN:
-        PLAN["plan"] = order(ops)
-    pre, start, end, eng = PLAN["plan"]
-    seq = sorted(range(len(ops)), key=lambda i: (start[i], i))
+        PLAN["plan"] = plan(ops)
+    pre, seq, eng = PLAN["plan"][:3]
     close(ops, seq)
     place = {i: k for k, i in enumerate(seq)}
     queue = {"v": g.vector, "a": g.scalar, "p": g.tensor, "g": g, "s": g.sync}
@@ -684,7 +766,7 @@ def rank_program(g, core, T, topo):
             if ops[j]["kind"] == "c":
                 if not (e == "p" and eng[j] == "p") and place[j] > last.get(eng[j], (-1, 0))[0]:
                     last[eng[j]] = (place[j], j)
-            elif j not in known[e]:
+            elif j not in known[e] and not behind(ops, i, j):
                 known[e][j] = 1
                 lst.append(j)
         for f, (pl, j) in last.items():

import math
import numpy as np
from concourse.bass import DstId, RemoteDMATransfer
from concourse.mybir import AluOpType, ActivationFunctionType

ALU = AluOpType
ACT = ActivationFunctionType
P, GH, NR, RO = 1024, 256, 6, 3
G3, B2, B0, GO, B1, G2, TOP = 0, 256, 1280, 2304, 3584, 4608, 4864
OWN = [B0, B1, B2]
CAND = [GO, G2, G3]
BASE = [B0, B0, G3]
STOP = [B1, TOP, TOP]
OFF = [1536, 512]
BIG = 8192.0

bf, f32, i32, u16, f16 = "bfloat16", "float32", "int32", "uint16", "float16"
SCRATCH = {"MB": ("sbuf", [128, 16, 8, 16], bf)}
for _dt, _list in (
        (bf, "GX 8192 GY 8192 GZ 8192 W0 3584 W1 4864 W2 4864 UW 4864 FT 4864 DTa 2304 DTb 2304 HL 2304 RW 1024 "
             "VN 1024 MT 256 LT 1024 E 128 ID 128 LM 128 NL 128 PEN 128 EN 128 MS 128 "
             "NG 128 ZB 144 ZK 144 ZG 144 ZH 144 ZA 144 ZC 144 ZP 144 ZM 144 EM 144 EP 144 CH 512 CM 512 CN 64"),
        (f32, "F 4864 FO 9216 X0 1024 X1 1024 VP 1024 TG0 256 TG1 256 TG2 256 TS0 256 TS1 256 TS2 256 TM 256 "
              "COL 16 OH 4 GM 8 IL 64 KY 320 ZZ 320 AC 64"),
        (i32, "SI 1024 AI 1024 IK 128 IK2 128 II 144 IZ 72 IM 64 IP 8 IO 4 GI 64 GJ 64 AJ 64 AK 64"),
        (u16, "HU0 512 HU1 512 CU 512 GL 64 KL 320 DR 64 D1 64 D2 64 LA 64 LB 64 FL 1024"),
        (f16, "ZR 1152 I16 128 R0 144 R1 144 H0 512 H1 512 TT 512 C16 512 CG 1024 B16 1024 DG0 1024 DG1 1024 DG2 1024 SV 64")):
    _w = _list.split()
    for _k in range(0, len(_w), 2):
        SCRATCH[_w[_k]] = ("sbuf", [128, int(_w[_k + 1])], _dt)
PSUM = ("A0", "A1", "B0", "B1", "P4", "P5", "P6", "P7")
for _k in PSUM:
    SCRATCH[_k] = ("psum", [128, 512], f32)
SEMAPHORES = (["cv", "ca", "cp", "cg"] + ["arV%d" % t for t in range(RO)] + ["arT%d" % t for t in range(RO)]
              + ["d%d" % k for k in range(80)])

CG, CPE, LAT, OVH, CDMA, CREM = 1.55, 0.5, 150.0, 70.0, 2400.0, 3000.0
CASES = [(1.6, 1.1, 1.2, 0.35, 150.0), (1.2, 1.0, 1.0, 0.25, 150.0), (2.0, 1.2, 3.0, 0.4, 200.0)]
ORDERS, SHAKES, MOVES, SEED, HEAT = 12, 250, 15000, 3, 100.0
CHUNKS = [(0, 384), (384, 896), (896, 1024)]
BANKS = [("A0", "B0"), ("A1", "B1"), ("P6", "P7")]
STEPS = ["k0", "k1", "c0", "c1", "k2", "c2"]
CANDS = [(0, 1024)]
GCH, XCH, YCH = 64, 128, 128
WAYS = "avavv"
KORD = [4, 0, 2, 1, 3]
KBANK = ["P6", "P4", "P7", "P6", "P4"]
FIN = [2, 8, 14, 0, 4, 6, 10, 12, 5, 11, 1, 3, 7, 9, 13, 15]
SLOTS = [("FO", P * _k) for _k in range(9)] + [("X0", 0), ("X1", 0), ("VP", 0)]
KEEP = True
PLAN = {}


def _conf(a, b):
    return a[0] == b[0] and a[1] < b[2] and b[1] < a[2] and (a[3] is None or b[3] is None or a[3] == b[3])


def build(g, core, T, topo):
    rank = T.rank_of(core)
    ops, sent = [], [None]
    V, S, PE = g.vector, g.scalar, g.tensor

    def reg(x):
        return x if len(x) == 4 else (x[0], x[1], x[2], None)

    def op(eng, cost, fn, r, w, kind="c", after=None, sem=None, inc=1, cls=None):
        ops.append({"eng": eng, "cost": cost, "fn": fn, "r": [reg(x) for x in r], "w": [reg(x) for x in w],
                    "kind": kind, "after": after, "sem": sem, "inc": inc, "cls": cls})
        return len(ops) - 1

    def ap(x):
        return T[x[0]][:, x[1]:x[2]]

    def two(x):
        return SCRATCH[x[0]][2] in (bf, u16, f16)

    def ts(out, in_, s1, s2, o0, o1=None):
        n = in_[2] - in_[1]
        c = max(64, n * (0.5 if two(out) and two(in_) else 1.0)) + OVH
        a1 = ap(s1) if isinstance(s1, tuple) else s1
        a2 = ap(s2) if isinstance(s2, tuple) else s2
        if o1 is None:
            fn = lambda e: V.tensor_scalar(ap(out), ap(in_), a1, None, o0)
        else:
            fn = lambda e: V.tensor_scalar(ap(out), ap(in_), a1, a2, o0, o1)
        return op("v", c, fn, [in_] + [x for x in (s1, s2) if isinstance(x, tuple)], [out])

    def cp(out, in_):
        n = in_[2] - in_[1]
        c = max(64, n * (0.5 if two(out) and two(in_) else 1.0)) + OVH
        return op("v", c, lambda e: V.tensor_copy(ap(out), ap(in_)), [in_], [out])

    def tt(out, a, b, o):
        n = a[2] - a[1]
        c = max(64, n * (1 if a[0] in PSUM or b[0] in PSUM else 2)) + OVH
        return op("v", c, lambda e: V.tensor_tensor(ap(out), ap(a), ap(b), o), [a, b], [out])

    def act(out, in_, func, bias):
        return op("a", max(64, in_[2] - in_[1]) + OVH, lambda e: S.activation(ap(out), ap(in_), func, bias=bias), [in_], [out])

    def scale(out, in_, col):
        return op("a", in_[2] - in_[1] + OVH, lambda e: S.activation(ap(out), ap(in_), ACT.Identity, scale=ap(col)),
                  [in_, col], [out])

    def move(out, in_, add=0.0):
        def fn(e):
            if e == "v":
                return V.tensor_scalar(ap(out), ap(in_), add, None, ALU.add)
            return S.activation(ap(out), ap(in_), ACT.Identity, bias=add)
        return op("va", in_[2] - in_[1] + OVH, fn, [in_], [out])

    def times(out, in_, mul, add=0.0):
        def fn(e):
            if e == "v":
                return V.tensor_scalar(ap(out), ap(in_), mul, add, ALU.mult, ALU.add)
            return S.activation(ap(out), ap(in_), ACT.Identity, bias=add, scale=mul)
        return op("va", in_[2] - in_[1] + OVH, fn, [in_], [out])

    def gat(out, win, off, eng="va"):
        def fn(e):
            src = ap(win).indirect(ap(off))
            if e == "v":
                return V.tensor_copy(ap(out), src)
            return S.activation(ap(out), src, ACT.Copy)
        return op(eng, (out[2] - out[1]) * CG + OVH, fn, [win, off], [out], cls="g")

    def gat2(out, win, off):
        for h in range(2):
            gat((out[0], out[1] + 512 * h, out[1] + 512 * h + 512), win, (off[0], off[1] + 32 * h, off[1] + 32 * h + 32))

    def gtt(out, win, off, b, o):
        return op("v", (out[2] - out[1]) * CG + OVH,
                  lambda e: V.tensor_tensor(ap(out), ap(win).indirect(ap(off)), ap(b), o), [win, off, b], [out], cls="g")

    def mm(items, r, bank, step=1):
        me = len(ops)

        def fn(e):
            last = None
            for k, (lo, hi, l, x, st) in enumerate(items):
                last = PE.matmul(T[bank][:, lo:hi:step], l, x, st, ops[me]["stop"] and k == len(items) - 1)
            return last
        c = sum(max(64, (it[1] - it[0] + step - 1) // step) for it in items) * CPE + OVH
        return op("p", c, fn, r, [(bank, min(it[0] for it in items), max(it[1] for it in items))],
                  cls=None if items[0][4] else "add")

    def tolist(bank, lo, z, src, tail=None):
        n = src[2] - src[1]
        it = [(lo, lo + n // 16, T[z][:, 15 - q:143 - q], T[src[0]][:, src[1] + q:src[2]:16], q == 0)
              for q in range(16)]
        r = [src, (z, 0, 144)]
        if tail is not None:
            it.append((lo, lo + n // 16, T[tail[0]][:, :], ap(tail[1]), False))
            r += [tail[1], (tail[0], 0, 128)]
        return mm(it, r, bank)

    def rowlist(bank, lo, o):
        h = "H%d" % (o % 2)
        z0 = 144 * (o // 2) + 14
        it = [(lo, lo + 64, T.ZR[:, z0 - 2 * u:z0 - 2 * u + 128], T[h][:, u:512:8], u == 0) for u in range(8)]
        return mm(it, [(h, 0, 512), ("ZR", 0, 1152)], bank)

    def fold(e, src, n0, n1, lo):
        r = T["R%d" % e]
        return [(lo, lo + (n1 - n0) // 2, r[:, 1 - h:129 - h], T[src][:, n0 + h:n1:2], h == 0) for h in range(2)]

    def dma(out, in_, r, w, eng="s"):
        q = {"s": g.sync, "a": g.scalar}[eng]
        return op(eng, CDMA, lambda e: q.dma_start(out, in_), r, w, kind="d", inc=16)

    def copy(out, in_):
        return dma(ap(out), ap(in_), [in_], [out])

    def again(buf, src, t):
        return copy((buf, CAND[t], CAND[t] + GH), (src, GO + GH * t, GO + GH * t + GH))

    def pool(out, n, pattern, base, cm, w, small=False):
        if small:
            fn = lambda e: g.iota(out, pattern, base, cm, allow_small_or_imprecise_dtypes=True)
        else:
            fn = lambda e: g.iota(out, pattern, base, cm)
        return op("g", 2 * n + 160, fn, [], [w, ("pool", 0, 1)], after=sent[0])

    def count(buf, lo, hi, base):
        return pool(T[buf][:, lo:hi], hi - lo, [[1, hi - lo]], base, 0, (buf, lo, hi), True)

    def fill(x, val):
        n = x[2] - x[1]
        return op("v", max(64, n * (0.5 if two(x) else 1.0)) + OVH, lambda e: V.memset(ap(x), val), [], [x])

    def send(src, dests, sem, land, cost):
        mask = topo.mask(core, dests[0][0])
        for d, _ in dests:
            mask &= topo.mask(core, d)
        ne = bin(mask).count("1")

        def fn(e, loc):
            ids = []
            for d, _ in dests:
                rid, pid = topo.addr(d, core)
                ids.append(DstId(rid=rid, pnc=pid))
            tr = RemoteDMATransfer(dst_ids=ids, dma_engine_mask=mask, remote_sem=T.sem[sem], src=ap(src),
                                   dsts=[x for _, x in dests])
            return g.remote_dma_fused([tr], local_sem=loc)
        k = op("g", cost, fn, [src], [], kind="r", inc=ne)
        op("x", 1, None, [], [land], kind="x", after=k, sem=sem, inc=ne * len(dests))

    def send_values(t, src):
        dests = [(T.cores[(rank - d) % NR], T["W%d" % t][:, GO + (d - 1) * GH:GO + d * GH]) for d in range(1, NR)]
        if t > 0:
            sent[0] = len(ops)
        send(src, dests, "arV%d" % t, ("W%d" % t, GO, B1), CREM + 4000)

    def send_tuples(t):
        send(("TS%d" % t, 0, 256), [(T.cores[(rank - t - 1) % NR], T["TG%d" % t][:, :])], "arT%d" % t,
             ("TG%d" % t, 0, 256), CREM + 1500)

    def col(k):
        return ("COL", k, k + 1)

    def selves(t):
        count("X%d" % (t % 2), 0, P, OWN[t] - B0 - OFF[(t + 1) % 2])

    dma(T.W0[:, B0:B0 + GH], T.v0[:, 0:GH], [], [("W0", B0, B0 + GH)])
    dma(T.SI[:, 0:GH], T.succ[:, 0:GH], [], [("SI", 0, GH)], eng="a")
    dma(T.W0[:, B0 + GH:GO], T.v0[:, GH:P], [], [("W0", B0 + GH, GO)])
    dma(T.SI[:, GH:P], T.succ[:, GH:P], [], [("SI", GH, P)], eng="a")
    dma(T.MT[:, :], T.mat[:, :], [], [("MT", 0, 256)])
    dma(T.VN[:, :], T.rew[:, :], [], [("VN", 0, P)], eng="a")
    pool(T.II[:, :], 144, [[-1, 144]], 0, 1, ("II", 0, 144))
    pool(T.IP[:, 0:1], 1, [[0, 1]], 0, 1, ("IP", 0, 1))
    pool(T.IK[:, :], 128, [[-16, 8], [0, 16]], 0, 1, ("IK", 0, 128))
    pool(T.IM[:, :], 64, [[16, 64]], 0, 0, ("IM", 0, 64))
    send_values(0, ("W0", B0, B0 + GH))
    pool(T.IZ[:, :], 72, [[-2, 8], [-16, 9]], 0, 1, ("IZ", 0, 72))
    selves(0)

    ts(("IP", 2, 3), ("IP", 0, 1), 15, None, ALU.bitwise_and)
    ts(("IP", 4, 5), ("IP", 0, 1), 1, None, ALU.bitwise_and)
    cp(col(1), ("IP", 4, 5))
    cp(col(0), ("IP", 2, 3))
    ts(col(2), col(1), -1.0, 1.0, ALU.mult, ALU.add)
    ts(col(3), col(1), float(OFF[0] - OFF[1]), float(-OFF[0]), ALU.mult, ALU.add)
    for e in range(2):
        ts(("R%d" % e, 0, 144), ("II", 0, 144), float(e - 1), col(2 - e), ALU.is_equal, ALU.mult)
    for n0, n1 in ((0, GH), (GH, P)):
        ts(("DG0", n0, n1), ("SI", n0, n1), col(3), None, ALU.add)
        for e in range(2):
            bank = "P%d" % (4 + e)
            mm(fold(e, "DG0", n0, n1, n0 // 2), [("R%d" % e, 0, 144), ("DG0", n0, n1)], bank)
            cp(("H%d" % e, n0 // 2, n1 // 2), (bank, n0 // 2, n1 // 2))
            ts(("HU%d" % e, n0 // 2, n1 // 2), ("H%d" % e, n0 // 2, n1 // 2), float(OFF[e]), None, ALU.add)
    ts(("TM", 0, 256), ("SI", 0, 256), float(GH), -BIG, ALU.is_ge, ALU.mult)
    tt(("TS1", 0, 256), ("TM", 0, 256), ("SI", 0, 256), ALU.add)
    move(("TS0", 0, 256), ("TS1", 0, 256), float(CAND[0] - B0 - OFF[1]))
    send_tuples(0)
    ts(("IK2", 0, 128), ("IK", 0, 128), 4, None, ALU.arith_shift_right)
    ts(("E", 0, 128), ("IK2", 0, 128), 0.0, None, ALU.is_equal)
    ts(("ID", 0, 128), ("II", 0, 128), 0.0, None, ALU.is_equal)
    cp(("I16", 0, 128), ("ID", 0, 128))
    op("v", 64 + OVH, lambda e: V.tensor_scalar(T.GM[:, :], T.E[:, 0:128:16], 1.0 / 256, None, ALU.mult),
       [("E", 0, 128)], [("GM", 0, 8)])
    for a in range(8):
        fn = lambda e, a=a: S.activation(T.MB[:, :, a, :], T.MT[:, :], ACT.Identity, scale=T.GM[:, a:a + 1])
        op("a", 256 + OVH, fn, [("MT", 0, 256), ("GM", 0, 8)], [("MB", a, a + 1)])
    act(("RW", 0, P), ("VN", 0, P), ACT.Identity, -128.0)
    mm([(0, 128, T.ID[:, :], T.MB[:, o, :, :], o == 0) for o in range(16)], [("ID", 0, 128), ("MB", 0, 8)], "P6")
    move(("MS", 0, 128), ("P6", 0, 128))
    ts(("IL", 0, 64), ("IM", 0, 64), col(0), None, ALU.add)
    fill(("ZB", 0, 144), 0.0)
    op("v", 64 + OVH, lambda e: V.tensor_copy(T.ZB[:, 15:143:16], T.E[:, 0:128:16]), [("E", 0, 128)], [("ZB", 0, 144)])
    fill(("ZR", 0, 1152), 0.0)
    for h in range(2):
        op("v", 72 + OVH, lambda e, h=h: V.tensor_scalar(T.ZR[:, 14 + h:1152:16], T.IZ[:, :], float(h), None, ALU.is_equal),
           [("IZ", 0, 72)], [("ZR", 0, 1152)])
    times(("ZK", 0, 144), ("ZB", 0, 144), 65536.0)
    times(("ZG", 0, 144), ("ZB", 0, 144), 1048576.0)
    times(("NG", 0, 128), ("ID", 0, 128), -1048576.0)
    ts(("IO", 0, 4), ("II", 0, 4), 15, None, ALU.bitwise_and)
    ts(("OH", 0, 4), ("IO", 0, 4), 0.0, None, ALU.is_equal)
    ts(col(4), ("OH", 0, 1), 64.0, ("OH", 1, 2), ALU.mult, ALU.add)
    for k, (z, row, wt) in enumerate((("ZA", 3, -2304.0), ("ZC", 3, 1024.0), ("ZP", 2, BIG), ("ZM", 2, -BIG))):
        ts(col(5 + k), ("OH", row, row + 1), wt, col(4), ALU.mult, ALU.add)
        scale((z, 0, 144), ("ZB", 0, 144), col(5 + k))
    scale(("ZH", 0, 144), ("ZB", 0, 144), col(4))
    scale(("EN", 0, 128), ("E", 0, 128), col(4))
    for z, wt in (("EM", -BIG), ("EP", BIG)):
        fill((z, 0, 144), 0.0)
        op("v", 64 + OVH, lambda e, z=z, wt=wt: V.tensor_scalar(T[z][:, 1:129:2], T.E[:, 0:128:2], wt, None, ALU.mult),
           [("E", 0, 128)], [(z, 0, 144)])
    times(("PEN", 0, 128), ("E", 0, 128), -BIG)
    times(("NL", 0, 128), ("ID", 0, 128), 4096.0)
    tt(("LM", 0, 128), ("NL", 0, 128), ("E", 0, 128), ALU.max)
    times(("NL", 0, 128), ("LM", 0, 128), -1.0)
    fill(("CH", 0, 512), -1280.0)
    fill(("CM", 0, 512), 128.0)
    times(("CN", 0, 64), ("E", 0, 64), 0.0, -983040.0)
    pool(T.HL[0:32, :], 2304, [[1, 36], [0, 64]], 0, 0, ("HL", 0, 2304, 0), True)
    pool(T.HL[32:64, :], 2304, [[0, 36], [1, 64]], 0, 0, ("HL", 0, 2304, 1), True)
    for r, cut in ((2, GH), (3, P)):
        pool(T.HL[32 * r:32 * r + 32, 0:cut], cut, [[0, cut]], 0, 0, ("HL", 0, cut, r), True)
        pool(T.HL[32 * r:32 * r + 32, cut:2304], 2304 - cut, [[0, 2304 - cut]], 1, 0, ("HL", cut, 2304, r), True)
    for r in range(4):
        dma(T.FT[r:128:4, B0:B1], T.HL[32 * r:32 * r + 32, :], [("HL", 0, 2304, r)], [("FT", B0, B1, r)])
    copy(("DTa", P, 2304), ("FT", GO, B1))
    copy(("DTb", P, 2304), ("FT", GO, B1))
    copy(("FT", B1, G2), ("FT", B0, GO))
    copy(("FT", B2, B0), ("FT", B0, GO))
    again("FT", "FT", 1)
    again("FT", "FT", 2)
    copy(("W2", B0, GO), ("W0", B0, GO))

    def guests():
        tt(("GI", 0, 64), ("P7", 0, 64), ("IL", 0, 64), ALU.add)
        ts(("GJ", 0, 64), ("GI", 0, 64), GH - 1, None, ALU.bitwise_and)
        cp(("GL", 0, 64), ("GJ", 0, 64))

    def lists(t, rows, bank, dst):
        off = float(OFF[rows[0] % 2] + B0 - BASE[t])
        for j, o in enumerate(rows):
            rowlist(bank, 64 * j, o)
        ts((dst[0], dst[1], dst[1] + 64 * len(rows)), (bank, 0, 64 * len(rows)), off, None, ALU.add)
        for j, o in enumerate(rows):
            if o % 3 == t and o // 3 < 5:
                k = o // 3
                act(("KY", 64 * k, 64 * k + 64), (bank, 64 * j, 64 * j + 64), ACT.Identity, off + 8192.0 * (5 - k))

    def klist(t, k):
        if t + 1 < RO:
            return "KL", 64 * [0, 3, 1, 4, 2][k]
        return "FL", 64 * FIN.index(3 * k + t)

    def early(t):
        lists(t, [t, t + 6, t + 12], "P4", ("KL", 0) if t + 1 < RO else ("FL", 0))

    def compose(buf, t):
        if t == 2:
            gat2((buf, B1, G2), (buf, B2, B1), ("LB", 0, 64))
        if t >= 1:
            gat2((buf, B0, GO), (buf, GO, G2), ("LA", 0, 64))

    def one_round(t):
        W, X, TG = "W%d" % t, "X%d" % (t % 2), "TG%d" % t
        par = (t + 1) % 2
        own = OWN[t]
        H, HU = "H%d" % par, "HU%d" % par
        if t == 0:
            for lo in range(GO, B1, 640):
                act(("UW", lo, lo + 640), (W, lo, lo + 640), ACT.Identity, -128.0)
        else:
            copy(("UW", GO, B1), (W, GO, B1))
            for u in range(1, t + 1):
                again(W, W, u)
                again("UW", W, u)

        def arcs(buf, lst, win, e, n0, n1, banks, most):
            for c0 in range(n0 // 2, n1 // 2, most):
                ch = min(most, n1 // 2 - c0)
                x = (buf, 16 * c0, 16 * (c0 + ch))
                gat(x, win, (lst, c0, c0 + ch))
                lo = 2 * c0 - n0
                for bank in banks:
                    mm([(lo + s % 2, lo + 2 * ch, T.MB[:, s - s % 2 + e, :, :], T[buf][:, x[1] + s:x[2]:16], False)
                        for s in range(16)], [x, ("MB", 0, 16)], bank, step=2)

        def kept(j):
            n0, n1 = CHUNKS[j]
            for bank in BANKS[j]:
                it = [(0, n1 - n0, T.ID[:, :], T.RW[:, n0:n1], True)]
                if t > 0:
                    it.append((0, n1 - n0, T.MS[:, :], T.CM[:, 0:n1 - n0], False))
                mm(it, [("ID", 0, 128), ("RW", n0, n1), ("MS", 0, 128), ("CM", 0, 512)][:2 * len(it)], bank)
            arcs("GX", "HU%d" % (1 - par), (W, B0, TOP if t == 2 else B1), 1 - par, n0, n1, BANKS[j], XCH)
            arcs("GY", HU, (W, B0, B1), par, n0, n1, BANKS[j][:1], YCH)
            ts(("AI", n0, n1), (BANKS[j][0], 0, n1 - n0), 127.25, -255.0 / 512, ALU.min, ALU.add)

        cw = [(B0, B1), (B1, TOP), (G3, B0)][t]

        def cands(j):
            n0, n1 = CANDS[j]
            gtt(("CG", n0, n1), (TG, 0, 256), ("GL", n0 // 16, n1 // 16), (X, n0, n1), ALU.min if t == 2 else ALU.max)
            mm(fold(par, "CG", n0, n1, n0 // 2), [("R%d" % par, 0, 144), ("CG", n0, n1)], "P5")
            if KEEP:
                cp(("C16", n0 // 2, n1 // 2), ("P5", n0 // 2, n1 // 2))
            ts(("CU", n0 // 2, n1 // 2), ("C16" if KEEP else "P5", n0 // 2, n1 // 2), float(OFF[par] + B0 - cw[0]), None, ALU.add)

        def choose(j):
            n0, n1 = CHUNKS[j]
            w, x, y = n1 - n0, n0 // 2, n1 // 2
            a, b = BANKS[j]
            arcs("GZ", "CU", (W, cw[0], cw[1]), par, n0, n1, [b], GCH)
            mm([(0, w, T.ID[:, :], T.CH[:, 0:w], True)], [("ID", 0, 128), ("CH", 0, 512)], a)
            tt(("LT", n0, n1), (b, 0, w), ("AI", n0, n1), ALU.is_lt)
            ts(("B16", n0, n1), (b, 0, w), 127.25, 1280 - 255.0 / 512, ALU.min, ALU.add)
            mm([(0, w, T.PEN[:, :], T.LT[:, n0:n1], False)], [("PEN", 0, 128), ("LT", n0, n1)], a)
            mm([(0, w, T.I16[:, :], T.B16[:, n0:n1], False)], [("I16", 0, 128), ("B16", n0, n1)], a)
            vc = ("UW", own + n0, own + n1)
            tt(vc, (a, 0, w), ("AI", n0, n1), ALU.max)
            move(("VP", n0, n1), vc, 1.0 / 16)
            if t + 1 == RO:
                move(("VN", n0, n1), vc, 128.0)
                dma(T.yv[:, n0:n1], T.VN[:, n0:n1], [("VN", n0, n1)], [])
            else:
                if n0 == 0:
                    send_values(t + 1, ("UW", own, own + GH))
                    selves(t + 1)
                    if t == 0:
                        count("F", GO, B1, P)
                        count("F", G2, TOP, P + GH)
                        count("F", G3, B2, P + 2 * GH)
                copy(("W%d" % (t + 1), OWN[t + 1] + n0, OWN[t + 1] + n1), vc)
            steps = [[("EM", "TT", H, ALU.max), ("EP", H, "TT", ALU.min)], [("EM", H, H, ALU.max)], [("EP", H, H, ALU.min)]][t]
            for u, (z, _, _, _) in enumerate(steps):
                it = fold(par, "CG", n0, n1, 256 * u)
                if KEEP:
                    it = [(256 * u, 256 * u + w // 2, T.I16[:, :], T.C16[:, x:y], True)]
                it += [(256 * u, 256 * u + w // 2, T[z][:, 1 - h:129 - h], T.LT[:, n0 + h:n1:2], False) for h in range(2)]
                mm(it, [("R%d" % par, 0, 144), ("C16", x, y) if KEEP else ("CG", n0, n1), (z, 0, 144), ("LT", n0, n1)], b)
            for u, (_, out, in1, o) in enumerate(steps):
                tt((out, x, y), (b, 256 * u, 256 * u + w // 2), (in1, x, y), o)
            if t + 1 < RO:
                ts((HU, x, y), (H, x, y), float(OFF[par]), None, ALU.add)

        for j in range(len(CANDS)):
            cands(j)
        for step in STEPS:
            (kept if step[0] == "k" else choose)(int(step[1]))
        tolist("P7", 0, "ZB", ("UW", own, own + P))
        cp(("SV", 0, 64), ("P7", 0, 64))
        if t + 1 < RO:
            guests()
        compose("UW", t)
        lists(t, [t + 3, t + 9], "P5", ("KL", 192) if t + 1 < RO else ("FL", 512))
        acc = ("IL", 0, 64)
        if own != BASE[t]:
            acc = ("AC", 0, 64)
            act(acc, ("IL", 0, 64), ACT.Identity, float(own - BASE[t]))
        uw = ("UW", BASE[t], STOP[t])
        for j, k in enumerate(KORD):
            bank, c, way = KBANK[j], 128 + 64 * k, WAYS[k]
            kb, kc = klist(t, k)
            u = WAYS[:k].count(way)
            if way == "a":
                df, sg = 2048 + P * u, P * u
                for lo in (0, 512):
                    hi, bk = lo + 512, ("A0", "A1", "B0", "B1")[2 * u + lo // 512]
                    mm([(0, 512, T.NL[:, :], T.UW[:, own + lo:own + hi], True)], [("NL", 0, 128), ("UW", own + lo, own + hi)], bk)
                    x = ("GZ", sg + lo, sg + hi)
                    gat(x, uw, (kb, kc + lo // 16, kc + hi // 16), eng="a")
                    mm([(0, 512, T.LM[:, :], ap(x), False)], [("LM", 0, 128), x], bk)
                    act(("GZ", df + lo, df + hi), (bk, 0, 512), ACT.Sign, -0.5)
                tolist(bank, c, "ZK", ("GZ", df, df + P), tail=("ID", ("CN", 0, 64)))
            else:
                df = "DG%d" % u
                gtt((df, 0, P), uw, (kb, kc, kc + 64), ("VP", 0, P), ALU.min)
                tolist(bank, c, "ZG", (df, 0, P), tail=("NG", ("SV", 0, 64)))
            tt(("ZZ", 64 * k, 64 * k + 64), (bank, c, c + 64), ("KY", 64 * k, 64 * k + 64), ALU.min)
            nxt = ("AJ", 0, 64) if j == 4 else ("P5", 448, 512)
            tt(nxt, acc, ("ZZ", 64 * k, 64 * k + 64), ALU.max)
            acc = nxt
        ts(("AK", 0, 64), ("AJ", 0, 64), 8191, None, ALU.bitwise_and)
        cp(("DR", 0, 64), ("AK", 0, 64))
        gat2(("DTa", 0, P), ("FT", BASE[t], STOP[t]), ("DR", 0, 64))
        d1 = ("DR", 0, 64)
        if t > 0:
            tolist("P6", 448, "ZH", ("DTa", 0, P))
            d1 = ("D1", 0, 64)
            cp(d1, ("P6", 448, 512))
        if t + 1 < RO:
            early(t + 1)
        else:
            lists(t, FIN[3:8], "P4", ("FL", 192))
            lists(t, FIN[10:16], "P5", ("FL", 640))
        gat2(("DTb", 0, P), ("DTa", 0, 2304), d1)
        tolist("P6", 448, "ZH", ("DTb", 0, P))
        cp(("D2", 0, 64), ("P6", 448, 512))
        if t + 1 < RO:
            gat2(("FT", own, own + P), ("DTb", 0, 2304), ("D2", 0, 64))
            if t == 0:
                tolist("P7", 448, "ZA", ("FT", own, own + P))
                ts(("LA", 0, 64), ("P7", 448, 512), 1280.0, None, ALU.add)
            else:
                tolist("P7", 448, "ZC", ("FT", own, own + P))
                cp(("LB", 0, 64), ("P7", 448, 512))
                gat2(("FT", B0, GO), ("FT", GO, G2), ("LA", 0, 64))
            compose("W%d" % (t + 1), t + 1)
            for h in range(2):
                gat(("GZ", 4096 + P * h, 5120 + P * h), ("FT", B0, B1), ("HU%d" % (1 - par), 64 * h, 64 * h + 64))
            z = "ZM" if t == 0 else "ZP"
            it = []
            for s in range(16):
                o = s - s % 2 + 1 - par
                it.append((64 + s % 2, 320, T[z][:, 15 - o:143 - o], T.GZ[:, 4096 + s:6144:16], s == 0))
            mm(it, [(z, 0, 144), ("GZ", 4096, 6144)], "P7", step=2)
            move(("TS%d" % (t + 1), 0, 256), ("P7", 64, 320), float(CAND[t + 1] - B0 - OFF[1 - par]))
            send_tuples(t + 1)
        else:
            for b in range(2):
                mm([(0, 512, T.EN[:, :], T.DTb[:, 512 * b:512 * b + 512], True)], [("EN", 0, 128), ("DTb", 512 * b, 512 * b + 512)],
                   "A%d" % b)
                move(("F", B0 + 512 * b, B0 + 512 * b + 512), ("A%d" % b, 0, 512))
            gat2(("F", B2, B0), ("F", B0, B1), ("D2", 0, 64))
            compose("F", t)

    tolist("P7", 0, "ZB", ("W0", B0, GO))
    guests()
    early(0)
    for t in range(RO):
        one_round(t)
    for j, o in enumerate(FIN):
        buf, s = SLOTS[j % len(SLOTS)]
        for lo, hi in ((0, P),) if j < 14 else ((0, 512), (512, P)):
            gat((buf, s + lo, s + hi), ("F", G3, TOP), ("FL", 64 * j + lo // 16, 64 * j + hi // 16))
            dma(T.ys[o:128:16, lo:hi], T[buf][0:128:16, s + lo:s + hi], [(buf, s + lo, s + hi)], [])
    return ops


def needs(ops):
    pre = [set() for _ in ops]
    seen = {}
    for i, o in enumerate(ops):
        if o["after"] is not None:
            pre[i].add(o["after"])
        for x, wr in [(x, False) for x in o["r"]] + [(x, True) for x in o["w"]]:
            lst = seen.setdefault(x[0], [])
            if x[0] in PSUM:
                for j, y, wy in reversed(lst):
                    add = ops[j]["cls"] == "add"
                    if not (add and o["cls"] == "add"):
                        pre[i].add(j)
                    if not add:
                        break
                continue
            for j, y, wy in lst:
                if (wr or wy) and _conf(x, y):
                    pre[i].add(j)
        for x in o["r"]:
            seen[x[0]].append((i, x, False))
        for x in o["w"]:
            seen[x[0]].append((i, x, True))
    return [sorted(x) for x in pre]


def behind(ops, i, j):
    return ops[i]["kind"] == "c" and ops[i]["after"] == j


def plan(ops):
    made = [order(ops, SEED + k, MOVES, HEAT) for k in range(ORDERS)]
    cuts = [i for i, o in enumerate(ops) if o["w"] and o["w"][0][0] == "DR"]

    def join(which):
        seq, pick, done = [], [None] * len(ops), set()
        for s, k in enumerate(which):
            other = made[k][1]
            for i in other[:other.index(cuts[s]) + 1] if s < len(cuts) else other:
                if i not in done:
                    done.add(i)
                    seq.append(i)
                    pick[i] = made[k][2][i]
        return order(ops, SEED, 0, HEAT, (seq, pick))

    which = [min(range(ORDERS), key=lambda k: made[k][4])] * (len(cuts) + 1)
    best = join(which)
    for s in range(len(which)):
        for k in range(ORDERS):
            w2 = which[:s] + [k] + which[s + 1:]
            r = join(w2)
            if r[4] < best[4]:
                which, best = w2, r
    return order(ops, SEED, MOVES, HEAT / 2, (best[1], best[2]))


def order(ops, seed, moves, heat, given=None):
    n = len(ops)
    pre = needs(ops)
    engs = [o["eng"] for o in ops]
    suc = [[] for _ in range(n)]
    for i in range(n):
        for j in pre[i]:
            suc[j].append(i)

    def case(cg, near, far, lat):
        cost = [(o["cost"] - OVH) * cg / CG + OVH if o["cls"] == "g" else
                {"d": o["cost"] * near, "r": CREM * near + (o["cost"] - CREM) * far}.get(o["kind"], o["cost"]) for o in ops]
        hold = [{"c": c, "d": 1200.0 if o["eng"] == "g" else 100.0, "r": 600.0, "x": 0.0}[o["kind"]] for o, c in zip(ops, cost)]
        near = [[(j, hold[j] if behind(ops, i, j) else cost[j] + (0.0 if engs[i] == "p" and engs[j] == "p" else lat))
                 for j in pre[i]] for i in range(n)]
        return cost, hold, near

    cases = [case(c[0], c[1], c[2], c[4]) for c in CASES]
    cost, hold, fw = cases[0]
    bw = [[] for _ in range(n)]
    for i in range(n):
        for j, d in fw[i]:
            bw[j].append((i, d + hold[i] - hold[j]))

    def place(key, near, first, back):
        key = list(key)
        for i in (range(n - 1, -1, -1) if back else range(n)):
            for j, d in near[i]:
                if key[j] >= key[i]:
                    key[i] = key[j] + 1e-3
        busy = {e: ([], []) for e in "vapgsx"}
        start, pick = [0.0] * n, [None] * n
        for i in sorted(range(n), key=lambda i: key[i]):
            s0, h, got = first[i], hold[i], None
            for j, d in near[i]:
                if start[j] + d > s0:
                    s0 = start[j] + d
            for e in engs[i]:
                a, b = busy[e]
                s, m = s0, len(a)
                k = m
                while k and b[k - 1] > s:
                    k -= 1
                while k < m and s + h > a[k]:
                    if b[k] > s:
                        s = b[k]
                    k += 1
                if got is None or s <= got[0] + 300.0:
                    got = (s, k, e)
            s, k, e = got
            pick[i], start[i] = e, s
            busy[e][0].insert(k, s)
            busy[e][1].insert(k, s + h)
        return start, pick

    def forward(key):
        st, pk = place(key, fw, [0.0] * n, False)
        return st, pk, max(st[i] + cost[i] for i in range(n))

    late = [cost[i] - hold[i] for i in range(n)]
    best = cur = forward(range(n))
    rnd = np.random.RandomState(seed)
    for it in range(0 if given else SHAKES):
        c, w = rnd.rand() * best[2], 3000 + rnd.rand() * 12000
        noise = ((rnd.rand(n) - 0.5) * 3000).tolist()
        key = [-(s + hold[i] + (noise[i] if abs(s - c) < w else 0.0)) for i, s in enumerate(cur[0])]
        sb, _ = place(key, bw, late, True)
        r = forward([-(sb[i] + hold[i]) for i in range(n)])
        if r[2] <= cur[2] + 400.0 * (1 - it / SHAKES):
            cur = r
            if r[2] < best[2]:
                best = r

    def replay(seq, pick, cs, old, a):
        cost, hold, near = cs
        free, last = dict.fromkeys("vapgsx", 0.0), dict.fromkeys("vapgsx", -1)
        start, why = list(old[1]), list(old[2])
        todo = 5
        for k in range(a - 1, -1, -1):
            i = seq[k]
            e = pick[i]
            if last[e] < 0 and e != "x":
                free[e], last[e] = start[i] + hold[i], i
                todo -= 1
                if not todo:
                    break
        top, ti = 0.0, -1
        for i in seq[a:]:
            e = pick[i]
            t, w = free[e], last[e]
            for j, d in near[i]:
                if start[j] + d > t:
                    t, w = start[j] + d, j
            start[i], why[i] = t, w
            if e != "x":
                free[e], last[e] = t + hold[i], i
            if t + cost[i] > top:
                top, ti = t + cost[i], i
        return top, start, why, ti

    def score(seq, pick, old, a):
        rs = [replay(seq, pick, cs, r, min(a, n - 40)) for cs, r in zip(cases, old)]
        return sum(r[0] * c[3] for r, c in zip(rs, CASES)), rs

    seq, pick = given or (sorted(range(n), key=lambda i: (best[0][i], i)), best[1])
    cur, rs = score(seq, pick, [(0, [0.0] * n, [-1] * n)] * len(cases), 0)
    best = (cur, seq, pick, rs)
    either = [m for m in range(n) if len(engs[m]) > 1]
    for it in range(moves):
        r = rs[rnd.randint(len(rs))]
        i, pairs = r[3], []
        while r[2][i] >= 0:
            j = r[2][i]
            if j not in pre[i]:
                pairs.append((j, i))
            i = j
        j, i = pairs[rnd.randint(len(pairs))]
        how = rnd.randint(6)
        s2, p2 = seq, pick
        if how < 2:
            k = (i, j)[how]
            if len(engs[k]) < 2:
                continue
            p2 = list(pick)
            p2[k] = "a" if p2[k] == "v" else "v"
            a = seq.index(k)
            if rnd.rand() < 0.5:
                c = [m for m in either if pick[m] == p2[k] and abs(r[1][m] - r[1][k]) < 4000]
                if c:
                    m = c[rnd.randint(len(c))]
                    p2[m] = pick[k]
                    a = min(a, seq.index(m))
        else:
            a, b = seq.index(j), seq.index(i)
            if how < 4:
                a = max(0, a - (rnd.randint(30) if how == 3 else 0))
                need, mv = set(pre[i]), [i]
                for m in reversed(seq[a:b]):
                    if m in need:
                        mv.append(m)
                        need.update(pre[m])
                ms = set(mv)
                s2 = seq[:a] + mv[::-1] + [m for m in seq[a:b] if m not in ms] + seq[b + 1:]
            else:
                b = min(n - 1, b + (rnd.randint(30) if how == 5 else 0))
                need, mv = set(suc[j]), [j]
                for m in seq[a + 1:b + 1]:
                    if m in need:
                        mv.append(m)
                        need.update(suc[m])
                ms = set(mv)
                s2 = seq[:a] + [m for m in seq[a + 1:b + 1] if m not in ms] + mv + seq[b + 1:]
        room = -math.log(1.0 - rnd.rand()) * (heat * (1 - it / moves) + 1)
        c2, r2 = 0.0, []
        for cs, r, c in zip(cases, rs, CASES):
            r2.append(replay(s2, p2, cs, r, min(a, n - 40)))
            c2 += (r2[-1][0] - r[0]) * c[3]
            if c2 > room + 150.0:
                break
        if c2 <= room:
            seq, pick, cur, rs = s2, p2, cur + c2, r2
            if cur < best[0]:
                best = (cur, seq, pick, rs)
    return pre, best[1], best[2], best[3], best[0]


def close(ops, seq):
    nxt = {}
    for i in reversed(seq):
        o = ops[i]
        for x in o["r"] + o["w"]:
            if x[0] in PSUM:
                o["stop"] = nxt.get(x[0]) != "add"
                nxt[x[0]] = o["cls"]


def rank_program(g, core, T, topo):
    if T.rank_of(core) is None:
        return
    ops = build(g, core, T, topo)
    if "plan" not in PLAN:
        PLAN["plan"] = plan(ops)
    pre, seq, eng = PLAN["plan"][:3]
    close(ops, seq)
    place = {i: k for k, i in enumerate(seq)}
    queue = {"v": g.vector, "a": g.scalar, "p": g.tensor, "g": g, "s": g.sync}
    need, marked, known = {}, set(), {e: {} for e in queue}
    for i in seq:
        if ops[i]["kind"] == "x":
            continue
        e, lst, last = eng[i], [], {}
        for j in pre[i]:
            if ops[j]["kind"] == "c":
                if not (e == "p" and eng[j] == "p") and place[j] > last.get(eng[j], (-1, 0))[0]:
                    last[eng[j]] = (place[j], j)
            elif j not in known[e] and not behind(ops, i, j):
                known[e][j] = 1
                lst.append(j)
        for f, (pl, j) in last.items():
            if known[e].get(f, -1) < pl:
                known[e][f] = pl
                marked.add(j)
                lst.append(j)
        need[i] = lst
    count, total, nd = {}, {}, 0
    for i in seq:
        o = ops[i]
        if o["kind"] == "c":
            if i in marked:
                s = "c" + eng[i]
                total[s] = total.get(s, 0) + 1
                count[i] = (s, total[s])
        else:
            if o["kind"] == "x":
                s = o["sem"]
            else:
                s = "d%d" % nd
                nd += 1
            total[s] = o["inc"]
            count[i] = (s, o["inc"])
    for i in seq:
        o = ops[i]
        if o["kind"] == "x":
            continue
        for j in need[i]:
            queue[eng[i]].wait_ge(T.sem[count[j][0]], count[j][1])
        if o["kind"] == "r":
            o["fn"](eng[i], T.sem[count[i][0]])
        else:
            ins = o["fn"](eng[i])
            if i in count:
                ins.then_inc(T.sem[count[i][0]], o["inc"])
    for s in sorted(total):
        g.sync.wait_ge(T.sem[s], total[s])
